import numpy as np, ml_dtypes
CORES = [16,17,18,19,32,33,34,35]
N = 8
BF = ml_dtypes.bfloat16
def f(rng, *shape):
    return (rng.standard_normal(shape, dtype=np.float32) * np.exp2(rng.integers(-2, 3, shape[:-1] + (1,)))).astype(BF)
def wide(rng, *shape):
    v = f(rng, *shape).astype(np.float32); k = shape[:-2] + (1, shape[-1])
    return (v * np.exp2(rng.integers(-6, 7, k)) * (rng.random(k) > 0.0625)).astype(BF)
M, K, TR, CAP = 4096, 32, 6, 128
D = 16 * K
def hashes(s, n):
    lo = ((s & 4095) + 1597 * n) & 4095; b = ((s >> 12) + ((lo * lo) >> 6)) & 4095
    return (lo + ((b * b) >> 6)) & 4095, b
def seed_of(a, b, n):
    lo = (a - ((b * b) >> 6)) & 4095
    return ((b - ((lo * lo) >> 6)) & 4095) * 4096 + ((lo - 1597 * n) & 4095)
def owners(t, s):
    a, b = hashes(np.asarray(s, np.int64)[..., None], (TR + 1) * np.arange(K)); w = (a * N) >> 12
    return np.where(b < t[w], w, t[N + w]).astype(np.int64)
def loads(t, s):
    o = owners(t, s); return np.stack([np.sum(o == q, -1) for q in range(N)], -1)
def sixteen(rng, t, keep=()):
    m = 16 - len(keep); kept = np.array(keep, np.int64); base = np.sum(loads(t, kept), 0)
    pool = rng.integers(0, 1 << 24, 1024); c = loads(t, pool); ok = np.flatnonzero(np.all(c * m <= CAP - base, 1)); j = np.arange(m)
    for u in range(m):
        if np.all(np.sum(c[j], 0) + base <= CAP): break
        j[u] = rng.choice(ok)
    return rng.permutation(np.concatenate([pool[j], kept]))
def ranks(rng, least):
    return np.concatenate([rng.integers(least, 4097, N), rng.permutation(N)]).astype(np.int64)
def absent(rng):
    w = rng.permutation(N); t = np.zeros(2 * N, np.int64)
    t[w] = (8192 * np.arange(N) + N - 1) // (2 * (N - 1)); t[N + w] = np.roll(w, -1); return t
def history(rng, dens):
    w = np.zeros((N, 128, M), np.float32)
    for q in range(N):
        for r in range(N):
            w[q] += np.float32(2 ** r) * (rng.random((128, M), dtype=np.float32) < dens[r][:, None])
    return w.astype(BF)
def seeds(rng, rk):
    return np.stack([np.stack([sixteen(rng, rk[g]) for g in range(8)]) for r in range(N)])
def complete(rng, rk, sd, dens=None):
    if dens is None: dens = rng.choice(np.array([0.1, 0.5, 0.9]), (N, 128))
    return {"sd": np.reshape(sd, (N, 128, 1)).astype(np.int32), "rk": np.stack([rk] * N).astype(np.int32), "thr": rng.integers(0, 4097, (N, 8, M)).astype(np.int32),
            "ali": rng.integers(0, M, (N, 8, M)).astype(np.int32), "seen": history(rng, dens), "vec": f(rng, N, 128, M)}
def setup_inputs(rng):
    rk = np.stack([ranks(rng, 2800) for g in range(8)]); return complete(rng, rk, seeds(rng, rk))
def setup_inputs_full(rng):
    o0 = rng.integers(0, N); rk = []
    for g in range(8):
        o = (o0 + g) % N; t = np.concatenate([rng.integers(3604 - 40, 3604 + 41, N), np.full(N, o)]).astype(np.int64); t[o] = 4096; rk.append(t)
    rk = np.stack(rk); sd = seeds(rng, rk); C = CAP // 16
    far = rng.integers(0, N, 8); h = rng.permutation(8); far[h[0]] = 0; far[h[1]] = rng.integers(1, N)
    for g in range(8):
        o = (o0 + g) % N; r = (o + far[g]) % N
        pool = rng.integers(0, 1 << 24, 4096); c = loads(rk[g], pool); fine = np.all(np.delete(c, o, 1) <= C, 1); s = []
        for i in range(8):
            x = rng.integers(-2, 3)
            for v in (C + x, C - x): s.append(pool[rng.choice(np.flatnonzero(fine & (c[:, o] == v)))])
        sd[r, g] = rng.permutation(np.array(s))
    return complete(rng, rk, sd)
def setup_inputs_edges(rng):
    rk, tie = [], []
    for g in range(8):
        t = ranks(rng, 3500); w = rng.permutation(N)[:4]; t[w[0]] = 0; t[N + w[0]] = w[1]; t[w[1]] = 0; t[N + w[1]] = w[0]; t[w[2]] = rng.integers(3500, 4096); t[N + w[2]] = w[0]; t[w[3]] = 4096; rk.append(t)
        tie.append(seed_of(int(w[2]) * (4096 // N) + int(rng.integers(0, 4096 // N)), int(t[w[2]]), (TR + 1) * int(rng.integers(0, K))))
    rk = np.stack(rk); sd = np.stack([np.stack([sixteen(rng, rk[g], (0, (1 << 24) - 1, tie[g])) for g in range(8)]) for r in range(N)])
    d = complete(rng, rk, sd); z = rng.integers(0, 4, (N, 8, M)); thr = np.where(z == 0, 0, np.where(z == 1, 4096, d["thr"])); z = rng.integers(0, 4, (N, 8, M))
    ali = np.where(z == 0, 0, np.where(z == 1, M - 1, np.where(z == 2, np.arange(M), d["ali"])))
    for r in range(N):
        for g in range(8):
            q = owners(rk[g], sd[r, g])[:, ::4]; a, b = hashes(sd[r, g][:, None], ((TR + 1) * np.arange(K) + 1)[None, ::4]); e = (a * M) >> 12
            thr[q, g, e] = b; ali[q, g, e] = M - 1 - e
    d["thr"] = thr.astype(np.int32); d["ali"] = ali.astype(np.int32); return d
def setup_inputs_hot(rng):
    rk = np.stack([ranks(rng, 2800) for g in range(8)]); sd = seeds(rng, rk)
    for g in range(8):
        pool = rng.integers(0, 1 << 24, 1024); sd[rng.integers(0, N), g] = pool[rng.choice(np.flatnonzero(np.all(loads(rk[g], pool) <= CAP // 16, 1)))]
    d = complete(rng, rk, sd); h = rng.integers(0, M, (N, 8, 1)); h[:, 0] = 0; h[:, 7] = M - 1
    d["thr"] = rng.integers(0, 512, (N, 8, M)).astype(np.int32); d["ali"] = (h + np.zeros((1, 1, M), np.int64)).astype(np.int32); return d
def setup_inputs_avid(rng):
    rk = np.stack([absent(rng) for g in range(8)]); dens = rng.choice(np.array([0, 0.97, 1.0]), (N, 128)); dens[rng.integers(0, N)] = 1
    return complete(rng, rk, seeds(rng, rk), dens)
def setup_inputs_spread(rng):
    d = setup_inputs(rng); d["vec"] = wide(rng, N, 128, M); d["thr"] = (4096 >> rng.integers(0, 14, (N, 8, M))).astype(np.int32); return d
def check_inputs(d):
    bad = []
    try:
        sd, rk = d["sd"].astype(np.int64), d["rk"].astype(np.int64); w = d["seen"].astype(np.float32)
        if not ((sd >= 0) & (sd < 1 << 24)).all(): bad.append("seed")
        if not (rk == rk[:1]).all(): bad.append("rk alike on all ranks")
        if not ((rk[..., :N] >= 0) & (rk[..., :N] <= 4096) & (rk[..., N:] >= 0) & (rk[..., N:] < N)).all(): bad.append("rk")
        if not ((d["thr"] >= 0) & (d["thr"] <= 4096)).all(): bad.append("thr")
        if not ((d["ali"] >= 0) & (d["ali"] < M)).all(): bad.append("ali")
        if not ((w >= 0) & (w < 2 ** N) & (w == np.floor(w))).all(): bad.append("seen")
        if not np.isfinite(d["vec"].astype(np.float32)).all(): bad.append("finite")
        if not bad and any((np.sum(loads(rk[r, g], sd[r, 16 * g:16 * g + 16, 0]), 0) > CAP).any() for r in range(N) for g in range(8)): bad.append("cap")
    except Exception:
        bad.append("unreadable")
    return bad
def reference(sd, rk, thr, ali, seen, vec):
    chosen = np.zeros((N, 128, K), np.float32); y = np.zeros((N, 128, D), vec.dtype); n = (TR + 1) * np.arange(K); row = np.arange(16)[:, None]
    for r in range(N):
        for g in range(8):
            s = sd[r, 16 * g:16 * g + 16].astype(np.int64)
            q = owners(rk[r, g].astype(np.int64), s[:, 0])
            x = np.zeros((16, K), np.int64); done = np.zeros((16, K), bool)
            for i in range(1, TR + 1):
                a, b = hashes(s, n + i); e = (a * M) >> 12
                c = np.where(b < thr[q, g, e], e, ali[q, g, e]).astype(np.int64)
                known = (seen[q, 16 * g + row, c].astype(np.float32).astype(np.int64) >> r) & 1
                x = np.where(done, x, c); done = done | (known == 0)
            chosen[r, 16 * g:16 * g + 16] = q * M + x
            y[r, 16 * g:16 * g + 16] = vec[q.T.reshape(-1), 16 * g + row, x.T.reshape(-1)]
    return {"chosen": chosen, "y": y}

@@ -1,0 +1,459 @@
+from concourse.bass import DstId, RemoteDMATransfer
+from concourse.mybir import AluOpType as A_, ActivationFunctionType as AF
+
+N = 8
+TRY = 6
+RW = 144
+BIG = float(1 << 23)
+OPS = {"+": A_.add, "-": A_.subtract, "*": A_.mult, "min": A_.min, ">=": A_.is_ge, ">": A_.is_gt, "<": A_.is_lt, "==": A_.is_equal,
+       ">>": A_.arith_shift_right, "&": A_.bitwise_and}
+
+SMALL = {
+    "bufI": ("int32", 8, "ckN 32 pI 8 p16I 8 sdI 8 hI 8 rkI 16 oT 32 oL 32 oL2 32 oSq 32 oB0 32 oB 32 oSr 32 oA0 32 oA 32 oW 32 yI 32 "
+             "oTh 32 oD 32 v 32 v5 32 aI 32 req 128 reqR 128 thrI 256 aliI 256 thH 256 thL 256 hs 64 H6 384 hT 384 hL 384 hL2 384 hq 384 "
+             "hb 384 hB 384 hr 384 ha 384 hA 384 hQ0 384 hQ 384 xI 384 cI 384 dI 320 wI 320 sI 320 pr 320 mI 320 acc 320 qI 64 q1 32 "
+             "q16 32 ps 32 mm 32 cq 32 cl 32 bl 32"),
+    "bufF": ("float32", 8, "ones 128 ckX 512 p16F 8 e8a 128 e8 128 wc 8 g9a 16 g9 16 selF 144 selF16 144 qc 8 w0 8 w2 8 w3 8 w4 8 wcol 8 "
+             "bcol 8 ya 8 yb 8 yc 16 dy 8 dyS 8 sF 8 hF 8 t8 256 t4 128 t2 64 oF 32 oFd 32 own 32 l1 32 be 32 beR 32 b8 256 b4 128 b2 64 "
+             "b1 32 rhsS 512 inX 512 wrS 64 wrK 64 lo 8 hi 8 q4k 32 ch1 32 ch2 32"),
+    "bufB": ("bfloat16", 16, "onesB 128 lta 128 lt 128 selB 144 selT 144 iotaS 128 ohI 512 oh 512 rs 256 mq 256 sc 256 l8 256 l4 128 "
+             "l2 64 alH 256 alL 256 thHb 256 thLb 256 mA 1024 mB 1024 mask 1024 m2 1024 cm 1024 ysb 512"),
+    "bufU": ("uint16", 16, "a16 32 e16 384 c16 320 f16 64 l16 160"),
+}
+SCRATCH = {}
+TILES = {}
+for _buf, (_type, _step, _list) in SMALL.items():
+    _at, _w = 0, _list.split()
+    for _n, _c in zip(_w[0::2], _w[1::2]):
+        TILES[_n] = (_buf, _at, int(_c))
+        _at += -(-int(_c) // _step) * _step
+    SCRATCH[_buf] = ("sbuf", [128, _at], _type)
+for _n, _c, _type in (("seenB", 4096, "bfloat16"), ("vecB", 4096, "bfloat16"), ("tabs", 4096, "bfloat16"), ("win", 1024, "float32"),
+                      ("tg", 6144, "bfloat16"), ("sg", 5120, "bfloat16"), ("rspR", N * RW, "bfloat16")):
+    SCRATCH[_n] = ("sbuf", [128, _c], _type)
+    TILES[_n] = (_n, 0, _c)
+for _j in range(8):
+    SCRATCH["p%d" % _j] = ("psum", [128, 512], "float32")
+    TILES["p%d" % _j] = ("p%d" % _j, 0, 512)
+SCRATCH["rsp"] = ("sbuf", [128, N, RW], "bfloat16")
+SEMAPHORES = ("sv ss sp sg d_sd d_rk d_thr d_ali d_seen d_vec d_tab0 d_tab1 d_tab2 d_tab3 d_ws d_wk d_y d_ch "
+              "l_be l_req l_off l_on r_be r_req r_rsp").split()
+
+
+def engine_plan(core, T, topo):
+    off = [c for c in T.cores if topo.chip(c) != topo.chip(core)]
+    on = [c for c in T.cores if topo.chip(c) == topo.chip(core) and c != core]
+    plan = {}
+    pool = topo.engines(core, off[0])
+    rest = [e for e in topo.engines(core, on[0]) if e not in pool]
+    for cores, engines in ((off, pool), (on, rest)):
+        n = 1
+        while 2 * n * len(cores) <= len(engines):
+            n *= 2
+        at = 0
+        for j, c in enumerate(cores):
+            m = n
+            if len(engines) - at - 2 * n >= n * (len(cores) - j - 1):
+                m = 2 * n
+            plan[c] = engines[at:at + m]
+            at += m
+    return plan, off, on
+
+
+def rank_program(g, core, T, topo):
+    me = T.rank_of(core)
+    if me is None:
+        return
+    queues = {"V": (g.vector, "sv"), "S": (g.scalar, "ss"), "P": (g.tensor, "sp"), "G": (g, "sg"), "Y": (g.sync, None)}
+    V, S, P, Y = g.vector, g.scalar, g.tensor, g.sync
+    count, waited, past = {}, {q: {} for q in queues}, {}
+
+    def X(spec):
+        if not isinstance(spec, str):
+            return spec
+        if "@" in spec:
+            w, o = spec.split("@")
+            (wa, wr), (oa, orr) = X(w), X(o)
+            return wa.indirect(oa), wr + orr
+        rows, name = (8, spec[2:]) if spec[:2] == "8|" else (128, spec)
+        f = name.split(":")
+        buf, at, n = TILES[f[0]]
+        a, b, st = (int(f[1]), int(f[2]), int(f[3]) if len(f) > 3 else 1) if len(f) > 1 else (0, n, 1)
+        lo, hi = (0, 512) if buf[0] == "p" and len(buf) == 2 else (at + a, at + b)
+        return T[buf][0:rows, at + a:at + b:st], [(buf, lo, hi, st)]
+
+    def meet(p, o):
+        return p[1] < o[2] and o[1] < p[2] and not (p[3] == o[3] and p[3] > 1 and (p[1] - o[1]) % p[3])
+
+    def need(q, reads, writes, part=None):
+        tok = {}
+        for places, wr in ((reads, False), (writes, True)):
+            for p in places:
+                for o, t, is_w, pt in past.get(p[0], []):
+                    if (is_w or (wr and t[0] != queues[q][1])) and meet(p, o) and (pt is None or part is None or pt == part):
+                        tok[t[0]] = max(tok.get(t[0], 0), t[1])
+        for s in sorted(tok):
+            if waited[q].get(s, 0) < tok[s]:
+                queues[q][0].wait_ge(T.sem[s], tok[s])
+                waited[q][s] = tok[s]
+
+    def note(tok, reads, writes, part=None):
+        for places, w in ((reads, False), (writes, True)):
+            for p in places:
+                past.setdefault(p[0], []).append((p, tok, w, part))
+
+    def run(q, call, out, ins, *more):
+        oa, ow = X(out)
+        reads, args = [], []
+        for i in ins:
+            if isinstance(i, (str, tuple)):
+                a, r = X(i)
+                args.append(a)
+                reads = reads + r
+            else:
+                args.append(i)
+        need(q, reads, ow)
+        s = queues[q][1]
+        count[s] = count.get(s, 0) + 1
+        call(oa, *args, *more).then_inc(T.sem[s], 1)
+        note((s, count[s]), reads, ow)
+
+    def ts(out, a, op, s1, op2=None, s2=None):
+        run("V", V.tensor_scalar, out, [a, s1, s2], *([OPS[op]] if op2 is None else [OPS[op], OPS[op2]]))
+
+    def tt(out, a, op, b):
+        run("V", V.tensor_tensor, out, [a, b], OPS[op])
+
+    def cp(out, a):
+        run("V", V.tensor_copy, out, [a])
+
+    def fill(out, c):
+        run("V", V.memset, out, [], c)
+
+    def act(out, a, scale=1.0, bias=None):
+        if bias is None:
+            run("S", lambda o, i, s: S.activation(o, i, AF.Copy, scale=s), out, [a, scale])
+        else:
+            run("S", lambda o, i, s, b: S.activation(o, i, AF.Identity, bias=b, scale=s), out, [a, scale, bias])
+
+    def iota(out, pattern, base, cm, exact=False):
+        run("G", lambda o: g.iota(o, pattern, base, cm) if exact else
+            g.iota(o, pattern, base, cm, allow_small_or_imprecise_dtypes=True), out, [])
+
+    def keep(out, a, pattern, op, base, cm):
+        run("G", lambda o, i: g.affine_select(o, i, pattern, OPS[op], 0.0, base, cm), out, [a])
+
+    def mms(out, pairs):
+        def call(o, *args):
+            for j in range(0, len(args), 2):
+                last = P.matmul(o, args[j], args[j + 1], j == 0, j == len(args) - 2)
+            return last
+        run("P", call, out, [x for p in pairs for x in p])
+
+    def dma(q, out, in_, sem, part=None):
+        (oa, ow), (ia, ir) = X(out), X(in_)
+        need(q, ir, ow, part)
+        queues[q][0].dma_start(oa, ia).then_inc(T.sem[sem], 16)
+        count[sem] = count.get(sem, 0) + 16
+        note((sem, count[sem]), ir, ow, part)
+
+    plan, off, on = engine_plan(core, T, topo)
+
+    def send(sem, dests, src, dst, local):
+        tr = []
+        for c in dests:
+            rid, pnc, _s = topo.addr(c)
+            a, r = X(src(T.rank_of(c)))
+            need("G", r, [])
+            m = 0
+            for e in plan[c]:
+                m |= 1 << e
+            tr.append(RemoteDMATransfer(dst_ids=[DstId(rid=rid, pnc=pnc)], dma_engine_mask=m, remote_sem=T.sem[sem],
+                                        srcs=[a], dsts=[X(dst)[0]], alu_op=0))
+            count[local] = count.get(local, 0) + len(plan[c])
+        g.remote_dma_fused(tr, local_sem=T.sem[local])
+
+    def landing(tile, width, sem):
+        count[sem] = sum(len(engine_plan(c, T, topo)[0][core]) for c in T.cores if c != core)
+        for r in range(N):
+            if r != me:
+                note((sem, count[sem]), [], X("%s:%d:%d" % (tile, width * r, width * r + width))[1])
+
+    def ext(t):
+        return (t[:], [])
+
+    landing("beR", 4, "r_be")
+    landing("reqR", 16, "r_req")
+    landing("rspR", RW, "r_rsp")
+
+    dma("Y", "sdI:0:1", ext(T.sd), "d_sd")
+    dma("S", "8|rkI", ext(T.rk), "d_rk")
+    dma("Y", "thrI", ext(T.thr), "d_thr")
+    dma("Y", "aliI", ext(T.ali), "d_ali")
+    dma("Y", "seenB", ext(T.seen), "d_seen")
+
+    for name, c in (("ones", 1.0), ("onesB", 1.0), ("selF", 0.0), ("rs", 1.0), ("be", 0.0), ("yc", 0.0), ("rs:0:256:32", 0.0), ("tabs", 0.0)):
+        fill(name, c)
+    step = 1597 * (TRY + 1)
+    iota("ckN", [[step, 32]], -int(BIG), 0, True)
+    iota("8|wc", [[-8192, 8]], 0, 0)
+    keep("8|e8a", "8|ones", [[1, 128]], ">=", 0, -16)
+    keep("8|e8", "8|e8a", [[-1, 128]], ">=", 15, 16)
+    iota("pI:0:1", [[0, 1]], 0, 1, True)
+    iota("ohI", [[0, 32], [1, 16]], 0, 0)
+    keep("g9a:0:9", "ones:0:9", [[-16, 9]], ">=", 0, 1)
+    keep("g9:0:9", "g9a:0:9", [[16, 9]], ">=", 15, -1)
+    iota("ckX", [[step, 32], [0, 16]], 0, 0)
+    keep("lta", "onesB", [[16, 8], [1, 16]], ">", 0, -1)
+    keep("lt", "lta", [[-16, 8], [0, 16]], ">=", 0, 1)
+    iota("qc", [[128, 8]], -1, 0)
+    iota("iotaS", [[1, 128]], 0, 0)
+
+    ts("8|ya", "8|rkI:8:16", "*", 8192.0)
+    tt("8|yb", "8|ya", "+", "8|wc")
+    tt("8|yc:1:9", "8|yb", "+", "8|rkI:0:8")
+    tt("8|dy", "8|yc:1:9", "-", "8|yc:0:8")
+    mms("p6:0:8", [("8|e8", "8|dy")])
+    act("dyS", "p6:0:8")
+
+    cp("sF:0:1", "sdI:0:1")
+    ts("hI:0:1", "sdI:0:1", ">>", 12)
+    ts("oT", "ckN", "+", "sF:0:1")
+    ts("hF:0:1", "hI:0:1", "*", 64.0, "+", -BIG)
+    ts("oL", "oT", "&", 4095)
+    ts("p16I:0:1", "pI:0:1", "&", 15)
+    tt("oSq", "oL", "*", "oL")
+    cp("p16F:0:1", "p16I:0:1")
+    ts("oB0", "oSq", "+", "hF:0:1")
+    ts("oL2", "oL", "*", 64.0, "+", -BIG)
+    ts("oB", "oB0", ">>", 6, "&", 4095)
+    ts("oh", "ohI", "==", "p16F:0:1")
+    tt("oSr", "oB", "*", "oB")
+    cp("selF:15:144:16", "g9:0:9")
+    tt("oA0", "oSr", "+", "oL2")
+    ts("bcol:0:1", "p16F:0:1", "==", 1.0, "*", -BIG)
+    ts("oA", "oA0", ">>", 6, "&", 4095)
+    ts("selF16", "selF", "*", 0.0625)
+    act("rhsS", "oh", "sF:0:1")
+    mms("p7", [("selF:15:143", "rhsS"), ("selF16:14:142", "ckX")])
+    act("inX", "p7", 1.0, "bcol:0:1")
+    act("win:0:512", "ckX", 0.0)
+    act("win:512:1024", "ckX", 0.0)
+
+    for w in range(N):
+        ts("t8:%d:%d" % (32 * w, 32 * w + 32), "oA", ">=", 512.0 * w, "*", "dyS:%d:%d" % (w, w + 1))
+    ts("oW", "oA", ">>", 9)
+    tt("t4", "t8:0:128", "+", "t8:128:256")
+    tt("t2", "t4:0:64", "+", "t4:64:128")
+    tt("yI", "t2:0:32", "+", "t2:32:64")
+    ts("oTh", "yI", "&", 8191)
+    ts("oD", "yI", ">>", 13)
+    tt("oF", "oB", ">=", "oTh")
+    tt("oFd", "oF", "*", "oD")
+    tt("own", "oFd", "+", "oW")
+    for q in range(N):
+        ts("mq:%d:%d" % (32 * q, 32 * q + 32), "own", "==", float(q))
+    run("V", V.tensor_tensor_scan, "sc", ["rs", "mq"], 0.0, A_.mult, A_.add)
+    mms("p6:16:24", [("lt", "sc:31:256:32")])
+    act("be:1:32:4", "sc:31:256:32")
+    tt("l8", "mq", "*", "sc")
+    tt("l4", "l8:0:128", "+", "l8:128:256")
+    tt("be:0:32:4", "p6:16:24", "+", "qc")
+    tt("l2", "l4:0:64", "+", "l4:64:128")
+    for q in range(N):
+        ts("b8:%d:%d" % (32 * q, 32 * q + 32), "own", "==", float(q), "*", "be:%d:%d" % (4 * q, 4 * q + 1))
+    tt("l1", "l2:0:32", "+", "l2:32:64")
+    tt("b4", "b8:0:128", "+", "b8:128:256")
+    tt("b2", "b4:0:64", "+", "b4:64:128")
+    tt("b1", "b2:0:32", "+", "b2:32:64")
+    tt("v", "b1", "+", "l1")
+    ts("v5", "v", "*", 1025.0)
+    ts("aI", "v5", ">>", 4, "&", 1023)
+    cp("a16", "aI")
+    mine4, mine16 = "%d:%d" % (4 * me, 4 * me + 4), "%d:%d" % (16 * me, 16 * me + 16)
+    send("r_be", off + on, lambda q: "be:%d:%d" % (4 * q, 4 * q + 4), "beR:" + mine4, "l_be")
+    cp("win@a16", "inX")
+    dma("Y", "wrS", (T.win[0:128:16, :], X("win")[1]), "d_ws")
+    dma("S", "wrK", (T.win[1:128:16, :], X("win")[1]), "d_wk")
+
+    cp("beR:" + mine4, "be:" + mine4)
+    cp("alH", "aliI")
+    ts("thH", "thrI", ">>", 8)
+    ts("thL", "thrI", "&", 255)
+    tt("alL", "aliI", "-", "alH")
+    ts("thHb", "thH", "+", -8.0)
+    cp("thLb", "thL")
+    for j, name in enumerate(("alL", "alH", "thLb", "thHb")):
+        dma("Y", (T.tabs[j:128:16, :], X("tabs")[1]), name, "d_tab%d" % j, j)
+    ts("w0:0:1", "p16F:0:1", "<", 2.0)
+    ts("w2:0:1", "p16F:0:1", "==", 2.0, "*", 8192.0)
+    ts("w3:0:1", "p16F:0:1", "==", 3.0, "*", 2097152.0)
+    cp("selB", "selF")
+    tt("w4:0:1", "w0:0:1", "+", "w2:0:1")
+    tt("wcol:0:1", "w4:0:1", "+", "w3:0:1")
+    ts("selT", "selF", "*", "wcol:0:1")
+
+    tt("req:0:128:2", "wrS", "+", "wrK")
+    cp("req:1:128:2", "wrS")
+    send("r_req", off + on, lambda q: "req:%d:%d" % (16 * q, 16 * q + 16), "reqR:" + mine16, "l_req")
+    cp("reqR:" + mine16, "req:" + mine16)
+    need("Y", X("wrS")[1], [])
+    dma("Y", "vecB", ext(T.vec), "d_vec")
+
+    ts("lo", "beR:0:32:4", "+", -float(128 * me - 1))
+    tt("hi", "lo", "+", "beR:1:32:4")
+    for m, c in (("mA", "lo"), ("mB", "hi")):
+        for r in range(N):
+            ts("%s:%d:%d" % (m, 128 * r, 128 * r + 128), "iotaS", ">=", "%s:%d:%d" % (c, r, r + 1), "*", float(2 ** (7 - r)))
+    tt("mask", "mA", "-", "mB")
+
+    ts("hs", "reqR:1:128:2", ">>", 12)
+
+    def hashes(i0, i1):
+        r = ":%d:%d" % (64 * i0, 64 * i1)
+        for i in range(i0, i1):
+            ts("hT:%d:%d" % (64 * i, 64 * i + 64), "reqR:0:128:2", "+", 1597.0 * (i + 1))
+        for i in range(i0, i1):
+            ts("H6:%d:%d" % (64 * i, 64 * i + 64), "hs", "*", 64.0, "+", -BIG)
+        ts("hL" + r, "hT" + r, "&", 4095)
+        tt("hq" + r, "hL" + r, "*", "hL" + r)
+        ts("hL2" + r, "hL" + r, "*", 64.0, "+", -BIG)
+        tt("hb" + r, "hq" + r, "+", "H6" + r)
+        ts("hB" + r, "hb" + r, ">>", 6, "&", 4095)
+        tt("hr" + r, "hB" + r, "*", "hB" + r)
+        tt("ha" + r, "hr" + r, "+", "hL2" + r)
+        ts("hA" + r, "ha" + r, ">>", 6, "&", 4095)
+        cp("e16" + r, "hA" + r)
+        ts("hQ0" + r, "hB" + r, "*", 8192.0, "+", 4096.0 - 16777216.0)
+        tt("hQ" + r, "hQ0" + r, "+", "hA" + r)
+
+    def R(i):
+        return ":%d:%d" % (64 * i, 64 * i + 64)
+
+    def wide(i):
+        return ":%d:%d" % (1024 * i, 1024 * i + 1024)
+
+    def wrap(out, sel, src, i):
+        mms(out + ":0:64", [("%s:%d:%d" % (sel, 15 - b, 143 - b), "%s:%d:%d:16" % (src, 1024 * i + b, 1024 * i + 1024)) for b in range(16)])
+
+    def table(i):
+        wrap("p%d" % (i % 3), "selT", "tg", i)
+
+    def item(i):
+        tt("xI" + R(i), "p%d:0:64" % (i % 3), "min", "hQ" + R(i))
+        ts("cI" + R(i), "xI" + R(i), "&", 4095)
+        if i < TRY - 1:
+            cp("c16" + R(i), "cI" + R(i))
+
+    def diff(i):
+        tt("dI" + R(i), "cI" + R(i + 1), "-", "cI" + R(i))
+
+    def seen(i):
+        tt("sg" + wide(i), "seenB@c16" + R(i), "*", "mask")
+        wrap("p%d" % (3 + i % 3), "selB", "sg", i)
+
+    def known(i):
+        cp("wI" + R(i), "p%d:0:64" % (3 + i % 3))
+        ts("sI" + R(i), "wI" + R(i), ">>", 7, "&", 1)
+
+    def go(i):
+        p = "sI" + R(0)
+        if i:
+            p = "pr" + R(i)
+            tt(p, ("pr" if i > 1 else "sI") + R(i - 1), "*", "sI" + R(i))
+        tt("mI" + R(i), p, "*", "dI" + R(i))
+        tt("acc" + R(i), "acc" + R(i - 1) if i else "cI" + R(0), "+", "mI" + R(i))
+
+    hashes(0, 1)
+    hashes(1, TRY)
+    for i in range(TRY):
+        act("tg" + wide(i), "tabs@e16" + R(i))
+    for i in range(3):
+        table(i)
+    item(0)
+    seen(0)
+    table(3)
+    item(1)
+    diff(0)
+    seen(1)
+    table(4)
+    known(0)
+    item(2)
+    go(0)
+    diff(1)
+    seen(2)
+    table(5)
+    known(1)
+    item(3)
+    go(1)
+    diff(2)
+    seen(3)
+    known(2)
+    item(4)
+    go(2)
+    diff(3)
+    seen(4)
+    item(5)
+    known(3)
+    diff(4)
+    go(3)
+    tt("qI", "pr" + R(3), "*", "dI" + R(4))
+    known(4)
+    tt("mI" + R(4), "sI" + R(4), "*", "qI")
+    tt("acc" + R(4), "acc" + R(3), "+", "mI" + R(4))
+    cp("f16", "acc" + R(4))
+
+    def block(r, a, b):
+        return T.rsp[:, r, a:b], [("rsp", RW * r + a, RW * r + b, 1)]
+
+    def parts(a, b):
+        return T.rsp[:, :, a:b], [("rsp", RW * r + a, RW * r + b, 1) for r in range(N)]
+
+    def features(q, r):
+        out = "rspR:%d:%d" % (RW * me, RW * me + 128) if r == me else block(r, 0, 128)
+        (act if q == "S" else cp)(out, "vecB@f16:%d:%d" % (8 * r, 8 * r + 8))
+
+    def answer(dests, local):
+        send("r_rsp", dests, lambda q: block(q, 0, RW), "rspR:%d:%d" % (RW * me, RW * me + RW), local)
+
+    offr = [T.rank_of(c) for c in off]
+    onr = [T.rank_of(c) for c in on] + [me]
+    features("S", offr[0])
+    cp(parts(136, 144), "acc" + R(4))
+    features("S", offr[1])
+    tt(parts(128, 136), "acc" + R(4), "-", parts(136, 144))
+    features("S", offr[2])
+    features("V", offr[3])
+    answer(off, "l_off")
+    features("S", onr[0])
+    features("V", onr[1])
+    features("S", onr[2])
+    answer(on, "l_on")
+    features("V", onr[3])
+    cp("rspR:%d:%d" % (RW * me + 128, RW * me + RW), block(me, 128, RW))
+
+    ts("q1", "v", ">>", 7)
+    ts("mm", "v", ">>", 4, "&", 7)
+    ts("bl", "v", "&", 15)
+    ts("q16", "q1", "*", float(RW - 128))
+    ts("cq", "q1", "*", float(RW), "+", 128.0)
+    ts("q4k", "q1", "*", 4096.0)
+    tt("ps", "v", "+", "q16")
+    tt("cl", "cq", "+", "mm")
+    cp("l16:0:32", "ps")
+    cp("l16:32:64", "cl")
+    ts("l16:64:96", "cl", "+", 8.0)
+    cp("l16:96:128", "bl")
+    cp("l16:128:160", "bl")
+    cp("m2", "oh:0:16@l16:96:160")
+
+    act("ysb", "rspR@l16:0:32")
+    dma("Y", ext(T.y), "ysb", "d_y")
+    tt("cm", "rspR@l16:32:96", "*", "m2")
+    mms("p7:0:64", [("selB:%d:%d" % (15 - u, 143 - u), "cm:%d:1024:16" % u) for u in range(16)])
+    tt("ch1", "p7:0:32", "+", "q4k")
+    tt("ch2", "p7:32:64", "+", "ch1")
+    dma("S", ext(T.chosen), "ch2", "d_ch")
+    for s in SEMAPHORES:
+        if count.get(s, 0) > waited["G"].get(s, 0):
+            g.wait_ge(T.sem[s], count[s])

@@ -10,15 +10,17 @@ OPS = {"+": A_.add, "-": A_.subtract, "*": A_.mult, "min": A_.min, ">=": A_.is_g
 
 SMALL = {
     "bufI": ("int32", 8, "ckN 32 pI 8 p16I 8 sdI 8 hI 8 rkI 16 oT 32 oL 32 oL2 32 oSq 32 oB0 32 oB 32 oSr 32 oA0 32 oA 32 oW 32 yI 32 "
-             "oTh 32 oD 32 v 32 v5 32 aI 32 req 128 reqR 128 thrI 256 aliI 256 thH 256 thL 256 hs 64 H6 384 hT 384 hL 384 hL2 384 hq 384 "
-             "hb 384 hB 384 hr 384 ha 384 hA 384 hQ0 384 hQ 384 xI 384 cI 384 dI 320 wI 320 sI 320 pr 320 mI 320 acc 320 qI 64 q1 32 "
-             "q16 32 ps 32 mm 32 cq 32 cl 32 bl 32"),
-    "bufF": ("float32", 8, "ones 128 ckX 512 p16F 8 e8a 128 e8 128 wc 8 g9a 16 g9 16 selF 144 selF16 144 qc 8 w0 8 w2 8 w3 8 w4 8 wcol 8 "
-             "bcol 8 ya 8 yb 8 yc 16 dy 8 dyS 8 sF 8 hF 8 t8 256 t4 128 t2 64 oF 32 oFd 32 own 32 l1 32 be 32 beR 32 b8 256 b4 128 b2 64 "
-             "b1 32 rhsS 512 inX 512 wrS 64 wrK 64 lo 8 hi 8 q4k 32 ch1 32 ch2 32"),
-    "bufB": ("bfloat16", 16, "onesB 128 lta 128 lt 128 selB 144 selT 144 iotaS 128 ohI 512 oh 512 rs 256 mq 256 sc 256 l8 256 l4 128 "
-             "l2 64 alH 256 alL 256 thHb 256 thLb 256 mA 1024 mB 1024 mask 1024 m2 1024 cm 1024 ysb 512"),
-    "bufU": ("uint16", 16, "a16 32 e16 384 c16 320 f16 64 l16 160"),
+             "oTh 32 oD 32 v 32 thrI 256 aliI 256 thH 256 thL 256 sT 64 hs 64 H6 384 hT 384 hL 384 hL2 384 "
+             "hb 384 hB 384 ha 384 hA 384 eI 384 xI 384 cI 384 dI 320 wI 320 sI 320 pr 320 mI 320 acc 320 qI 64 q1 32 "
+             "q16 32 ps 32 mm 32 cq 32 cl 32 bl 32 b8I 32 mb 32"),
+    "bufF": ("float32", 8, "ones 128 p16F 8 n16 8 e8a 128 e8 128 wc 8 g9a 16 g9 16 qc 8 w0 8 w1 8 w2 8 w3 8 w4 8 w5 8 w6 8 wcol 8 c3 8 "
+             "ya 8 yb 8 yc 16 dy 8 dyS 8 sF 8 hF 8 r1 8 t8 128 t4 64 oF 32 oFd 32 own 32 be 32 beR 32 b8 128 b4 64 "
+             "b2 64 y2 32 kk 384 lo 8 hi 8 q4k 32 ch1 32"),
+    "bufB": ("bfloat16", 16, "onesB 128 lta 128 lt 128 selB 144 selT 144 selA 144 selC 144 selK 144 sel0 128 sel1 128 sel2 128 "
+             "idn 128 up8 128 dn8 128 wI0 128 wI1 128 wU 128 wD 128 iH 64 iL 64 oh8 16 "
+             "x2 16 x1 16 x0 16 iotaS 128 ohI 512 ohA 512 oh 512 kX 512 inX 512 rs 256 mq 256 sc 256 alH 256 alL 256 thHb 256 thLb 256 "
+             "win 1024 mB 1024 mask 1024 m2 512 cm 512 ysb 512"),
+    "bufU": ("uint16", 16, "a16 32 e16 384 c16 320 f16 64 l16 96"),
 }
 SCRATCH = {}
 TILES = {}
@@ -28,16 +30,18 @@ for _buf, (_type, _step, _list) in SMALL.items():
         TILES[_n] = (_buf, _at, int(_c))
         _at += -(-int(_c) // _step) * _step
     SCRATCH[_buf] = ("sbuf", [128, _at], _type)
-for _n, _c, _type in (("seenB", 4096, "bfloat16"), ("vecB", 4096, "bfloat16"), ("tabs", 4096, "bfloat16"), ("win", 1024, "float32"),
+for _n, _c, _type in (("seenB", 4096, "bfloat16"), ("vecB", 4096, "bfloat16"), ("tabs", 4096, "bfloat16"),
                       ("tg", 6144, "bfloat16"), ("sg", 5120, "bfloat16"), ("rspR", N * RW, "bfloat16")):
     SCRATCH[_n] = ("sbuf", [128, _c], _type)
     TILES[_n] = (_n, 0, _c)
 for _j in range(8):
     SCRATCH["p%d" % _j] = ("psum", [128, 512], "float32")
     TILES["p%d" % _j] = ("p%d" % _j, 0, 512)
-SCRATCH["rsp"] = ("sbuf", [128, N, RW], "bfloat16")
-SEMAPHORES = ("sv ss sp sg d_sd d_rk d_thr d_ali d_seen d_vec d_tab0 d_tab1 d_tab2 d_tab3 d_ws d_wk d_y d_ch "
-              "l_be l_req l_off l_on r_be r_req r_rsp").split()
+BLOCKS = {"rq1": 16, "rq2": 32, "rr1": 16, "rr2": 32, "rsp": RW}
+for _n, _c in BLOCKS.items():
+    SCRATCH[_n] = ("sbuf", [128, N, _c], "bfloat16" if _n == "rsp" else "int32")
+SEMAPHORES = ("sv ss sp sg d_sd d_rk d_thr d_ali d_seen d_vec d_tab0 d_tab1 d_tab2 d_tab3 d_y d_ch "
+              "l_be l_rq1 l_rq2 l_rsp r_be r_rq1 r_rq2 r_rsp").split()
 
 
 def engine_plan(core, T, topo):
@@ -79,19 +83,23 @@ def rank_program(g, core, T, topo):
         f = name.split(":")
         buf, at, n = TILES[f[0]]
         a, b, st = (int(f[1]), int(f[2]), int(f[3]) if len(f) > 3 else 1) if len(f) > 1 else (0, n, 1)
-        lo, hi = (0, 512) if buf[0] == "p" and len(buf) == 2 else (at + a, at + b)
-        return T[buf][0:rows, at + a:at + b:st], [(buf, lo, hi, st)]
+        return T[buf][0:rows, at + a:at + b:st], [(buf, at + a, at + b, st)]
 
-    def meet(p, o):
-        return p[1] < o[2] and o[1] < p[2] and not (p[3] == o[3] and p[3] > 1 and (p[1] - o[1]) % p[3])
+    def meet(p, o, own):
+        if p[0][0] == "p" and not own:
+            return True
+        if p[1] >= o[2] or o[1] >= p[2]:
+            return False
+        return (p[3] == 1 and o[3] == 1) or bool(set(range(p[1], p[2], p[3])) & set(range(o[1], o[2], o[3])))
 
     def need(q, reads, writes, part=None):
-        tok = {}
+        tok, mine = {}, queues[q][1]
         for places, wr in ((reads, False), (writes, True)):
             for p in places:
                 for o, t, is_w, pt in past.get(p[0], []):
-                    if (is_w or (wr and t[0] != queues[q][1])) and meet(p, o) and (pt is None or part is None or pt == part):
-                        tok[t[0]] = max(tok.get(t[0], 0), t[1])
+                    if (is_w or wr or (p[0][0] == "p" and t[0] != mine)) and tok.get(t[0], 0) < t[1] \
+                            and meet(p, o, t[0] == mine) and (pt is None or part is None or pt == part):
+                        tok[t[0]] = t[1]
         for s in sorted(tok):
             if waited[q].get(s, 0) < tok[s]:
                 queues[q][0].wait_ge(T.sem[s], tok[s])
@@ -130,11 +138,14 @@ def rank_program(g, core, T, topo):
     def fill(out, c):
         run("V", V.memset, out, [], c)
 
-    def act(out, a, scale=1.0, bias=None):
-        if bias is None:
-            run("S", lambda o, i, s: S.activation(o, i, AF.Copy, scale=s), out, [a, scale])
-        else:
-            run("S", lambda o, i, s, b: S.activation(o, i, AF.Identity, bias=b, scale=s), out, [a, scale, bias])
+    def weave(*chains):
+        for j in range(max(len(c) for c in chains)):
+            for c in chains:
+                if j < len(c):
+                    c[j][0](*c[j][1:])
+
+    def act(out, a):
+        run("S", lambda o, i: S.activation(o, i, AF.Copy), out, [a])
 
     def iota(out, pattern, base, cm, exact=False):
         run("G", lambda o: g.iota(o, pattern, base, cm) if exact else
@@ -159,9 +170,9 @@ def rank_program(g, core, T, topo):
 
     plan, off, on = engine_plan(core, T, topo)
 
-    def send(sem, dests, src, dst, local):
+    def send(sem, src, dst, local):
         tr = []
-        for c in dests:
+        for c in off + on:
             rid, pnc, _s = topo.addr(c)
             a, r = X(src(T.rank_of(c)))
             need("G", r, [])
@@ -173,18 +184,31 @@ def rank_program(g, core, T, topo):
             count[local] = count.get(local, 0) + len(plan[c])
         g.remote_dma_fused(tr, local_sem=T.sem[local])
 
-    def landing(tile, width, sem):
+    def block(name, r, a=0, b=None):
+        w = BLOCKS[name]
+        b = w if b is None else b
+        return T[name][:, r, a:b], [(name, w * r + a, w * r + b, 1)]
+
+    def parts(name, a, b):
+        w = BLOCKS[name]
+        return T[name][:, :, a:b], [(name, w * r + a, w * r + b, 1) for r in range(N)]
+
+    def landing(piece, sem):
         count[sem] = sum(len(engine_plan(c, T, topo)[0][core]) for c in T.cores if c != core)
         for r in range(N):
             if r != me:
-                note((sem, count[sem]), [], X("%s:%d:%d" % (tile, width * r, width * r + width))[1])
+                note((sem, count[sem]), [], X(piece(r))[1])
 
     def ext(t):
         return (t[:], [])
 
-    landing("beR", 4, "r_be")
-    landing("reqR", 16, "r_req")
-    landing("rspR", RW, "r_rsp")
+    def at(name, w, i):
+        return "%s:%d:%d" % (name, w * i, w * i + w)
+
+    landing(lambda r: at("beR", 4, r), "r_be")
+    landing(lambda r: block("rr1", r), "r_rq1")
+    landing(lambda r: block("rr2", r), "r_rq2")
+    landing(lambda r: at("rspR", RW, r), "r_rsp")
 
     dma("Y", "sdI:0:1", ext(T.sd), "d_sd")
     dma("S", "8|rkI", ext(T.rk), "d_rk")
@@ -192,268 +216,277 @@ def rank_program(g, core, T, topo):
     dma("Y", "aliI", ext(T.ali), "d_ali")
     dma("Y", "seenB", ext(T.seen), "d_seen")
 
-    for name, c in (("ones", 1.0), ("onesB", 1.0), ("selF", 0.0), ("rs", 1.0), ("be", 0.0), ("yc", 0.0), ("rs:0:256:32", 0.0), ("tabs", 0.0)):
+    for name, c in (("ones", 1.0), ("onesB", 1.0), ("selB", 0.0), ("rs", 1.0), ("be", 0.0), ("yc", 0.0), ("rs:0:256:32", 0.0), ("tabs", 0.0)):
         fill(name, c)
     step = 1597 * (TRY + 1)
     iota("ckN", [[step, 32]], -int(BIG), 0, True)
     iota("8|wc", [[-8192, 8]], 0, 0)
-    keep("8|e8a", "8|ones", [[1, 128]], ">=", 0, -16)
-    keep("8|e8", "8|e8a", [[-1, 128]], ">=", 15, 16)
     iota("pI:0:1", [[0, 1]], 0, 1, True)
-    iota("ohI", [[0, 32], [1, 16]], 0, 0)
+    keep("8|e8a", "8|ones", [[1, 128]], ">=", 0, -16)
     keep("g9a:0:9", "ones:0:9", [[-16, 9]], ">=", 0, 1)
+    keep("8|e8", "8|e8a", [[-1, 128]], ">=", 15, 16)
     keep("g9:0:9", "g9a:0:9", [[16, 9]], ">=", 15, -1)
-    iota("ckX", [[step, 32], [0, 16]], 0, 0)
+    iota("ohI", [[0, 32], [1, 16]], 0, 0)
     keep("lta", "onesB", [[16, 8], [1, 16]], ">", 0, -1)
     keep("lt", "lta", [[-16, 8], [0, 16]], ">=", 0, 1)
     iota("qc", [[128, 8]], -1, 0)
+    iota("kX", [[1, 32], [0, 16]], 0, 0)
+    iota("win", [[0, 1024]], 0, 0)
     iota("iotaS", [[1, 128]], 0, 0)
-
-    ts("8|ya", "8|rkI:8:16", "*", 8192.0)
-    tt("8|yb", "8|ya", "+", "8|wc")
-    tt("8|yc:1:9", "8|yb", "+", "8|rkI:0:8")
-    tt("8|dy", "8|yc:1:9", "-", "8|yc:0:8")
-    mms("p6:0:8", [("8|e8", "8|dy")])
-    act("dyS", "p6:0:8")
 
     cp("sF:0:1", "sdI:0:1")
     ts("hI:0:1", "sdI:0:1", ">>", 12)
+    ts("8|ya", "8|rkI:8:16", "*", 8192.0)
     ts("oT", "ckN", "+", "sF:0:1")
     ts("hF:0:1", "hI:0:1", "*", 64.0, "+", -BIG)
+    tt("8|yb", "8|ya", "+", "8|wc")
     ts("oL", "oT", "&", 4095)
-    ts("p16I:0:1", "pI:0:1", "&", 15)
+    cp("x2:0:1", "sF:0:1")
+    tt("8|yc:1:9", "8|yb", "+", "8|rkI:0:8")
     tt("oSq", "oL", "*", "oL")
-    cp("p16F:0:1", "p16I:0:1")
+    ts("p16I:0:1", "pI:0:1", "&", 15)
+    tt("8|dy", "8|yc:1:9", "-", "8|yc:0:8")
     ts("oB0", "oSq", "+", "hF:0:1")
+    mms("p3:0:8", [("8|e8", "8|dy")])
+    act("dyS", "p3:0:8")
     ts("oL2", "oL", "*", 64.0, "+", -BIG)
+    cp("p16F:0:1", "p16I:0:1")
     ts("oB", "oB0", ">>", 6, "&", 4095)
-    ts("oh", "ohI", "==", "p16F:0:1")
+    ts("n16:0:1", "p16F:0:1", "*", -1.0)
+    run("S", lambda o, i, b: S.activation(o, i, AF.Abs, bias=b), "ohA", ["ohI", "n16:0:1"])
+    run("S", lambda o, i: S.activation(o, i, AF.Relu, bias=1.0, scale=-1.0), "oh", ["ohA"])
+    tt("r1:0:1", "sF:0:1", "-", "x2:0:1")
+    cp("selB:15:144:16", "g9:0:9")
     tt("oSr", "oB", "*", "oB")
-    cp("selF:15:144:16", "g9:0:9")
+    cp("x1:0:1", "r1:0:1")
+    ts("c3:0:1", "p16F:0:1", "==", 3.0)
     tt("oA0", "oSr", "+", "oL2")
-    ts("bcol:0:1", "p16F:0:1", "==", 1.0, "*", -BIG)
+    ts("selK", "selB", "*", 0.0625)
+    tt("x0:0:1", "r1:0:1", "-", "x1:0:1")
     ts("oA", "oA0", ">>", 6, "&", 4095)
-    ts("selF16", "selF", "*", 0.0625)
-    act("rhsS", "oh", "sF:0:1")
-    mms("p7", [("selF:15:143", "rhsS"), ("selF16:14:142", "ckX")])
-    act("inX", "p7", 1.0, "bcol:0:1")
-    act("win:0:512", "ckX", 0.0)
-    act("win:512:1024", "ckX", 0.0)
-
+    ts("sel2", "selB:13:141", "*", "x2:0:1")
+    ts("sel1", "selB:14:142", "*", "x1:0:1")
     for w in range(N):
-        ts("t8:%d:%d" % (32 * w, 32 * w + 32), "oA", ">=", 512.0 * w, "*", "dyS:%d:%d" % (w, w + 1))
+        ts(at("p0" if w < 4 else "t8", 32, w % 4), "oA", ">=", 512.0 * w, "*", at("dyS", 1, w))
     ts("oW", "oA", ">>", 9)
-    tt("t4", "t8:0:128", "+", "t8:128:256")
-    tt("t2", "t4:0:64", "+", "t4:64:128")
-    tt("yI", "t2:0:32", "+", "t2:32:64")
+    tt("p1:0:64", "p0:0:64", "+", "t8:0:64")
+    tt("t4", "p0:64:128", "+", "t8:64:128")
+    ts("sel0", "selB:15:143", "*", "x0:0:1")
+    tt("p0:128:160", "p1:0:32", "+", "t4:0:32")
+    tt("y2", "p1:32:64", "+", "t4:32:64")
+    tt("yI", "p0:128:160", "+", "y2")
+    mms("p7", [("sel%d" % j, "oh") for j in range(3)] + [("selK:12:140", "kX")])
+    act("inX", "p7")
     ts("oTh", "yI", "&", 8191)
     ts("oD", "yI", ">>", 13)
     tt("oF", "oB", ">=", "oTh")
+    ts("w0:0:1", "p16F:0:1", "<", 2.0)
     tt("oFd", "oF", "*", "oD")
+    ts("w2:0:1", "p16F:0:1", "==", 2.0, "*", 8192.0)
     tt("own", "oFd", "+", "oW")
+    ts("w1:0:1", "p16F:0:1", "<", 3.0)
     for q in range(N):
-        ts("mq:%d:%d" % (32 * q, 32 * q + 32), "own", "==", float(q))
+        ts(at("mq", 32, q), "own", "==", float(q))
+    ts("selC", "selB", "*", "c3:0:1")
     run("V", V.tensor_tensor_scan, "sc", ["rs", "mq"], 0.0, A_.mult, A_.add)
-    mms("p6:16:24", [("lt", "sc:31:256:32")])
+    mms("p2:0:8", [("lt", "sc:31:256:32")])
     act("be:1:32:4", "sc:31:256:32")
-    tt("l8", "mq", "*", "sc")
-    tt("l4", "l8:0:128", "+", "l8:128:256")
-    tt("be:0:32:4", "p6:16:24", "+", "qc")
-    tt("l2", "l4:0:64", "+", "l4:64:128")
+    ts("selA", "selB", "*", "w1:0:1")
+    tt("w4:0:1", "w0:0:1", "+", "w2:0:1")
+    tt("be:0:32:4", "p2:0:8", "+", "qc")
+    ts("w3:0:1", "c3:0:1", "*", 2097152.0)
     for q in range(N):
-        ts("b8:%d:%d" % (32 * q, 32 * q + 32), "own", "==", float(q), "*", "be:%d:%d" % (4 * q, 4 * q + 1))
-    tt("l1", "l2:0:32", "+", "l2:32:64")
-    tt("b4", "b8:0:128", "+", "b8:128:256")
-    tt("b2", "b4:0:64", "+", "b4:64:128")
-    tt("b1", "b2:0:32", "+", "b2:32:64")
-    tt("v", "b1", "+", "l1")
-    ts("v5", "v", "*", 1025.0)
-    ts("aI", "v5", ">>", 4, "&", 1023)
-    cp("a16", "aI")
-    mine4, mine16 = "%d:%d" % (4 * me, 4 * me + 4), "%d:%d" % (16 * me, 16 * me + 16)
-    send("r_be", off + on, lambda q: "be:%d:%d" % (4 * q, 4 * q + 4), "beR:" + mine4, "l_be")
+        ts(at("p1", 32, q), at("sc", 32, q), "+", "be:%d:%d" % (4 * q, 4 * q + 1))
+    tt("p0:0:128", "p1:0:128", "*", "mq:0:128")
+    tt("b8", "p1:128:256", "*", "mq:128:256")
+    tt("wcol:0:1", "w4:0:1", "+", "w3:0:1")
+    tt("p0:128:192", "p0:0:64", "+", "b8:0:64")
+    tt("b4", "p0:64:128", "+", "b8:64:128")
+    ts("selT", "selB", "*", "wcol:0:1")
+    tt("b2", "p0:128:192", "+", "b4")
+    tt("v", "b2:0:32", "+", "b2:32:64")
+    cp("a16", "v")
+    send("r_be", lambda q: at("be", 4, q), at("beR", 4, me), "l_be")
     cp("win@a16", "inX")
-    dma("Y", "wrS", (T.win[0:128:16, :], X("win")[1]), "d_ws")
-    dma("S", "wrK", (T.win[1:128:16, :], X("win")[1]), "d_wk")
+    for out, sel in (("p5:0:64", "selA"), ("p4:0:64", "selC")):
+        mms(out, [("%s:%d:%d" % (sel, 15 - b, 143 - b), "win:%d:1024:16" % b) for b in range(16)])
 
-    cp("beR:" + mine4, "be:" + mine4)
     cp("alH", "aliI")
     ts("thH", "thrI", ">>", 8)
     ts("thL", "thrI", "&", 255)
     tt("alL", "aliI", "-", "alH")
     ts("thHb", "thH", "+", -8.0)
     cp("thLb", "thL")
+    cp(at("beR", 4, me), at("be", 4, me))
     for j, name in enumerate(("alL", "alH", "thLb", "thHb")):
         dma("Y", (T.tabs[j:128:16, :], X("tabs")[1]), name, "d_tab%d" % j, j)
-    ts("w0:0:1", "p16F:0:1", "<", 2.0)
-    ts("w2:0:1", "p16F:0:1", "==", 2.0, "*", 8192.0)
-    ts("w3:0:1", "p16F:0:1", "==", 3.0, "*", 2097152.0)
-    cp("selB", "selF")
-    tt("w4:0:1", "w0:0:1", "+", "w2:0:1")
-    tt("wcol:0:1", "w4:0:1", "+", "w3:0:1")
-    ts("selT", "selF", "*", "wcol:0:1")
-
-    tt("req:0:128:2", "wrS", "+", "wrK")
-    cp("req:1:128:2", "wrS")
-    send("r_req", off + on, lambda q: "req:%d:%d" % (16 * q, 16 * q + 16), "reqR:" + mine16, "l_req")
-    cp("reqR:" + mine16, "req:" + mine16)
-    need("Y", X("wrS")[1], [])
     dma("Y", "vecB", ext(T.vec), "d_vec")
+    keep("idn", "onesB", [[-1, 128]], "==", 0, 1)
+    keep("up8", "onesB", [[-1, 128]], "==", 8, 1)
+    keep("dn8", "onesB", [[-1, 128]], "==", -8, 1)
 
-    ts("lo", "beR:0:32:4", "+", -float(128 * me - 1))
+    def R(name, i, n=1):
+        return "%s:%d:%d" % (name, 64 * i, 64 * i + 64 * n)
+
+    def hashes(i0, i1, name, beside):
+        n, m = i1 - i0, list(beside)
+
+        def other(k=1):
+            for _ in range(k):
+                if m:
+                    ts(*m.pop(0))
+
+        def r(tile):
+            return R(tile, i0, n)
+
+        for i in range(i0, i1):
+            ts(R("kk", i), "p4:0:64", "*", float(step), "+", 1597.0 * (i + 1) - BIG)
+        if i0 == 0:
+            cp("sT", "p5:0:64")
+        for i in range(i0, i1):
+            tt(R("hT", i), "p5:0:64", "+", R("kk", i))
+        if i0 == 0:
+            ts("hs", "sT", ">>", 12)
+        ts(r("hL"), r("hT"), "&", 4095)
+        for i in range(i0, i1):
+            ts(R("H6", i), "hs", "*", 64.0, "+", -BIG)
+        q, rr, q0 = R("p6", 0, n), R("p6", 4, n), "p7:0:%d" % (64 * n)
+        tt(q, r("hL"), "*", r("hL"))
+        ts(r("hL2"), r("hL"), "*", 64.0, "+", -BIG)
+        tt(r("hb"), q, "+", r("H6"))
+        other()
+        ts(r("hB"), r("hb"), ">>", 6, "&", 4095)
+        other()
+        tt(rr, r("hB"), "*", r("hB"))
+        ts(q0, r("hB"), "*", 8192.0, "+", 4096.0 - 16777216.0)
+        tt(r("ha"), rr, "+", r("hL2"))
+        other()
+        ts(r("hA"), r("ha"), ">>", 6, "&", 4095)
+        other()
+        for i in range(i0, i1):
+            tt(parts("rq" + name, 8 * (i - i0), 8 * (i - i0) + 8), R("p7", i - i0), "+", R("hA", i))
+        send("r_rq" + name, lambda q: block("rq" + name, q), block("rr" + name, me), "l_rq" + name)
+        other(len(m))
+        cp(block("rr" + name, me), block("rq" + name, me))
+
+    hashes(0, 2, "1", [])
+    hashes(2, TRY, "2", [("lo", "beR:0:32:4", "+", -float(128 * me - 1))] +
+           [(at("p0" if r < 4 else "p1", 128, r % 4), "iotaS", ">=", at("lo", 1, r), "*", float(2 ** (7 - r))) for r in range(N)])
     tt("hi", "lo", "+", "beR:1:32:4")
-    for m, c in (("mA", "lo"), ("mB", "hi")):
-        for r in range(N):
-            ts("%s:%d:%d" % (m, 128 * r, 128 * r + 128), "iotaS", ">=", "%s:%d:%d" % (c, r, r + 1), "*", float(2 ** (7 - r)))
-    tt("mask", "mA", "-", "mB")
+    for r in range(N):
+        ts(at("mB", 128, r), "iotaS", ">=", at("hi", 1, r), "*", float(2 ** (7 - r)))
 
-    ts("hs", "reqR:1:128:2", ">>", 12)
+    def packed(i):
+        return parts("rr1", 8 * i, 8 * i + 8) if i < 2 else parts("rr2", 8 * i - 16, 8 * i - 8)
 
-    def hashes(i0, i1):
-        r = ":%d:%d" % (64 * i0, 64 * i1)
+    def places(i0, i1):
         for i in range(i0, i1):
-            ts("hT:%d:%d" % (64 * i, 64 * i + 64), "reqR:0:128:2", "+", 1597.0 * (i + 1))
+            ts(R("eI", i), packed(i), "&", 4095)
         for i in range(i0, i1):
-            ts("H6:%d:%d" % (64 * i, 64 * i + 64), "hs", "*", 64.0, "+", -BIG)
-        ts("hL" + r, "hT" + r, "&", 4095)
-        tt("hq" + r, "hL" + r, "*", "hL" + r)
-        ts("hL2" + r, "hL" + r, "*", 64.0, "+", -BIG)
-        tt("hb" + r, "hq" + r, "+", "H6" + r)
-        ts("hB" + r, "hb" + r, ">>", 6, "&", 4095)
-        tt("hr" + r, "hB" + r, "*", "hB" + r)
-        tt("ha" + r, "hr" + r, "+", "hL2" + r)
-        ts("hA" + r, "ha" + r, ">>", 6, "&", 4095)
-        cp("e16" + r, "hA" + r)
-        ts("hQ0" + r, "hB" + r, "*", 8192.0, "+", 4096.0 - 16777216.0)
-        tt("hQ" + r, "hQ0" + r, "+", "hA" + r)
-
-    def R(i):
-        return ":%d:%d" % (64 * i, 64 * i + 64)
-
-    def wide(i):
-        return ":%d:%d" % (1024 * i, 1024 * i + 1024)
+            cp(R("e16", i), R("eI", i))
 
     def wrap(out, sel, src, i):
         mms(out + ":0:64", [("%s:%d:%d" % (sel, 15 - b, 143 - b), "%s:%d:%d:16" % (src, 1024 * i + b, 1024 * i + 1024)) for b in range(16)])
 
+    def bank(i):
+        return ("p2", "p6", "p7")[i % 3]
+
     def table(i):
-        wrap("p%d" % (i % 3), "selT", "tg", i)
-
-    def item(i):
-        tt("xI" + R(i), "p%d:0:64" % (i % 3), "min", "hQ" + R(i))
-        ts("cI" + R(i), "xI" + R(i), "&", 4095)
-        if i < TRY - 1:
-            cp("c16" + R(i), "cI" + R(i))
-
-    def diff(i):
-        tt("dI" + R(i), "cI" + R(i + 1), "-", "cI" + R(i))
+        wrap(bank(i), "selT", "tg", i)
 
     def seen(i):
-        tt("sg" + wide(i), "seenB@c16" + R(i), "*", "mask")
+        tt(at("sg", 1024, i), "seenB@" + R("c16", i), "*", "mask")
         wrap("p%d" % (3 + i % 3), "selB", "sg", i)
 
-    def known(i):
-        cp("wI" + R(i), "p%d:0:64" % (3 + i % 3))
-        ts("sI" + R(i), "wI" + R(i), ">>", 7, "&", 1)
+    def item(i):
+        ops = [(tt, R("xI", i), bank(i) + ":0:64", "min", packed(i)), (ts, R("cI", i), R("xI", i), "&", 4095)]
+        if i < TRY - 1:
+            ops.append((cp, R("c16", i), R("cI", i)))
+        return ops + ([(tt, R("dI", i - 1), R("cI", i), "-", R("cI", i - 1))] if i else [])
 
-    def go(i):
-        p = "sI" + R(0)
-        if i:
-            p = "pr" + R(i)
-            tt(p, ("pr" if i > 1 else "sI") + R(i - 1), "*", "sI" + R(i))
-        tt("mI" + R(i), p, "*", "dI" + R(i))
-        tt("acc" + R(i), "acc" + R(i - 1) if i else "cI" + R(0), "+", "mI" + R(i))
+    def known(j):
+        return [(cp, R("wI", j), "p%d:0:64" % (3 + j % 3)), (ts, R("sI", j), R("wI", j), ">>", 7, "&", 1)]
 
-    hashes(0, 1)
-    hashes(1, TRY)
-    for i in range(TRY):
-        act("tg" + wide(i), "tabs@e16" + R(i))
-    for i in range(3):
-        table(i)
-    item(0)
+    def go(j):
+        p = R("pr", j) if j else R("sI", 0)
+        return ([(tt, p, R("pr" if j > 1 else "sI", j - 1), "*", R("sI", j))] if j else []) + \
+            [(tt, R("mI", j), p, "*", R("dI", j)), (tt, R("acc", j), R("acc", j - 1) if j else R("cI", 0), "+", R("mI", j))]
+
+    places(0, 2)
+    act("tg:0:512", "tabs@e16:0:32")
+    cp("tg:512:1024", "tabs@e16:32:64")
+    table(0)
+    act("tg:1024:2048", "tabs@" + R("e16", 1))
+    table(1)
+    tt("mask:0:512", "p0", "-", "mB:0:512")
+    tt("mask:512:1024", "p1", "-", "mB:512:1024")
+    weave(item(0))
     seen(0)
-    table(3)
-    item(1)
-    diff(0)
+    places(2, TRY)
+    for i in range(2, TRY):
+        act(at("tg", 1024, i), "tabs@" + R("e16", i))
+    table(2)
+    weave(item(1))
     seen(1)
-    table(4)
-    known(0)
-    item(2)
-    go(0)
-    diff(1)
-    seen(2)
-    table(5)
-    known(1)
-    item(3)
-    go(1)
-    diff(2)
-    seen(3)
-    known(2)
-    item(4)
-    go(2)
-    diff(3)
-    seen(4)
-    item(5)
-    known(3)
-    diff(4)
-    go(3)
-    tt("qI", "pr" + R(3), "*", "dI" + R(4))
-    known(4)
-    tt("mI" + R(4), "sI" + R(4), "*", "qI")
-    tt("acc" + R(4), "acc" + R(3), "+", "mI" + R(4))
-    cp("f16", "acc" + R(4))
-
-    def block(r, a, b):
-        return T.rsp[:, r, a:b], [("rsp", RW * r + a, RW * r + b, 1)]
-
-    def parts(a, b):
-        return T.rsp[:, :, a:b], [("rsp", RW * r + a, RW * r + b, 1) for r in range(N)]
+    ts("w6:0:1", "p16F:0:1", "<", 8.0)
+    ts("w5:0:1", "p16F:0:1", ">=", 8.0)
+    for out, a, c in (("wI0", "idn", "w6"), ("wU", "up8", "w6"), ("wI1", "idn", "w5"), ("wD", "dn8", "w5")):
+        ts(out, a, "*", c + ":0:1")
+    tt("oh8:0:8", "oh:0:8", "+", "oh:8:16")
+    for i in range(2, TRY - 1):
+        table(i + 1)
+        weave(go(i - 3) if i > 2 else [], item(i), known(i - 2))
+        seen(i)
+    weave(go(2), item(5), known(3))
+    last = go(3)
+    weave(last[:2] + [(tt, "qI", R("pr", 3), "*", R("dI", 4)), (cp, R("wI", 4), "p4:0:64"), last[2], known(4)[1]])
+    tt(R("mI", 4), R("sI", 4), "*", "qI")
+    tt(R("acc", 4), R("acc", 3), "+", R("mI", 4))
+    cp("f16", R("acc", 4))
 
     def features(q, r):
-        out = "rspR:%d:%d" % (RW * me, RW * me + 128) if r == me else block(r, 0, 128)
-        (act if q == "S" else cp)(out, "vecB@f16:%d:%d" % (8 * r, 8 * r + 8))
+        out = "rspR:%d:%d" % (RW * me, RW * me + 128) if r == me else block("rsp", r, 0, 128)
+        (act if q == "S" else cp)(out, "vecB@" + at("f16", 8, r))
 
-    def answer(dests, local):
-        send("r_rsp", dests, lambda q: block(q, 0, RW), "rspR:%d:%d" % (RW * me, RW * me + RW), local)
-
-    offr = [T.rank_of(c) for c in off]
-    onr = [T.rank_of(c) for c in on] + [me]
-    features("S", offr[0])
-    cp(parts(136, 144), "acc" + R(4))
-    features("S", offr[1])
-    tt(parts(128, 136), "acc" + R(4), "-", parts(136, 144))
-    features("S", offr[2])
-    features("V", offr[3])
-    answer(off, "l_off")
-    features("S", onr[0])
-    features("V", onr[1])
-    features("S", onr[2])
-    answer(on, "l_on")
-    features("V", onr[3])
-    cp("rspR:%d:%d" % (RW * me + 128, RW * me + RW), block(me, 128, RW))
+    order = [T.rank_of(c) for c in off + on] + [me]
+    features("S", order[0])
+    cp("iH", R("acc", 4))
+    features("S", order[1])
+    features("S", order[2])
+    features("V", order[3])
+    tt("iL", R("acc", 4), "-", "iH")
+    mms("p2:0:64", [("wU", "iH"), ("wI0", "iL")])
+    mms("p2:64:128", [("wD", "iH"), ("wI1", "iL")])
+    features("S", order[4])
+    features("V", order[5])
+    for h in range(2):
+        cp(parts("rsp", 128 + 8 * h, 136 + 8 * h), "p2:%d:%d" % (64 * h, 64 * h + 64))
+    features("S", order[6])
+    send("r_rsp", lambda q: block("rsp", q), at("rspR", RW, me), "l_rsp")
+    features("V", order[7])
+    cp("rspR:%d:%d" % (RW * me + 128, RW * me + RW), block("rsp", me, 128, RW))
 
     ts("q1", "v", ">>", 7)
     ts("mm", "v", ">>", 4, "&", 7)
-    ts("bl", "v", "&", 15)
+    ts("bl", "v", "&", 7)
+    ts("b8I", "v", "&", 8)
     ts("q16", "q1", "*", float(RW - 128))
     ts("cq", "q1", "*", float(RW), "+", 128.0)
     ts("q4k", "q1", "*", 4096.0)
+    tt("mb", "mm", "+", "b8I")
     tt("ps", "v", "+", "q16")
-    tt("cl", "cq", "+", "mm")
+    cp("l16:64:96", "bl")
+    tt("cl", "cq", "+", "mb")
     cp("l16:0:32", "ps")
     cp("l16:32:64", "cl")
-    ts("l16:64:96", "cl", "+", 8.0)
-    cp("l16:96:128", "bl")
-    cp("l16:128:160", "bl")
-    cp("m2", "oh:0:16@l16:96:160")
+    cp("m2", "oh8:0:8@l16:64:96")
 
     act("ysb", "rspR@l16:0:32")
     dma("Y", ext(T.y), "ysb", "d_y")
-    tt("cm", "rspR@l16:32:96", "*", "m2")
-    mms("p7:0:64", [("selB:%d:%d" % (15 - u, 143 - u), "cm:%d:1024:16" % u) for u in range(16)])
+    tt("cm", "rspR@l16:32:64", "*", "m2")
+    mms("p7:0:32", [("selB:%d:%d" % (15 - u, 143 - u), "cm:%d:512:16" % u) for u in range(16)])
     tt("ch1", "p7:0:32", "+", "q4k")
-    tt("ch2", "p7:32:64", "+", "ch1")
-    dma("S", ext(T.chosen), "ch2", "d_ch")
+    dma("S", ext(T.chosen), "ch1", "d_ch")
     for s in SEMAPHORES:
         if count.get(s, 0) > waited["G"].get(s, 0):
             g.wait_ge(T.sem[s], count[s])

@@ -5,21 +5,21 @@ N = 8
 TRY = 6
 RW = 144
 BIG = float(1 << 23)
-OPS = {"+": A_.add, "-": A_.subtract, "*": A_.mult, "min": A_.min, ">=": A_.is_ge, ">": A_.is_gt, "<": A_.is_lt, "==": A_.is_equal,
-       ">>": A_.arith_shift_right, "&": A_.bitwise_and}
+OPS = {"+": A_.add, "-": A_.subtract, "*": A_.mult, "min": A_.min, "max": A_.max, ">=": A_.is_ge, ">": A_.is_gt, "<": A_.is_lt,
+       "==": A_.is_equal, ">>": A_.arith_shift_right, "&": A_.bitwise_and}
 
 SMALL = {
     "bufI": ("int32", 8, "ckN 32 pI 8 p16I 8 sdI 8 hI 8 rkI 16 oT 32 oL 32 oL2 32 oSq 32 oB0 32 oB 32 oSr 32 oA0 32 oA 32 oW 32 yI 32 "
-             "oTh 32 oD 32 v 32 thrI 256 aliI 256 thH 256 thL 256 sT 64 hs 64 H6 384 hT 384 hL 384 hL2 384 "
-             "hb 384 hB 384 ha 384 hA 384 eI 384 xI 384 cI 384 dI 320 wI 320 sI 320 pr 320 mI 320 acc 320 qI 64 q1 32 "
+             "oTh 32 oD 32 v 32 thrI 256 aliI 256 thH 256 thL 256 sT 64 hs 64 hT 384 hL 384 hL2 384 "
+             "hb 384 hB 384 ha 384 hA 384 eI 384 xI 384 cI 384 kI 320 wI 320 sI 320 acc 320 a6 64 aA 64 q1 32 "
              "q16 32 ps 32 mm 32 cq 32 cl 32 bl 32 b8I 32 mb 32"),
     "bufF": ("float32", 8, "ones 128 p16F 8 n16 8 e8a 128 e8 128 wc 8 g9a 16 g9 16 qc 8 w0 8 w1 8 w2 8 w3 8 w4 8 w5 8 w6 8 wcol 8 c3 8 "
              "ya 8 yb 8 yc 16 dy 8 dyS 8 sF 8 hF 8 r1 8 t8 128 t4 64 oF 32 oFd 32 own 32 be 32 beR 32 b8 128 b4 64 "
-             "b2 64 y2 32 kk 384 lo 8 hi 8 q4k 32 ch1 32"),
-    "bufB": ("bfloat16", 16, "onesB 128 lta 128 lt 128 selB 144 selT 144 selA 144 selC 144 selK 144 sel0 128 sel1 128 sel2 128 "
+             "b2 64 y2 32 kk 384 H6 384 ha2 8 nm 8 nm0 8 mT 1024 q4k 32 ch1 32"),
+    "bufB": ("bfloat16", 16, "onesB 128 lta 128 lt 128 selB 144 selT 144 selA 144 selC 144 selK 144 selX 128 "
              "idn 128 up8 128 dn8 128 wI0 128 wI1 128 wU 128 wD 128 iH 64 iL 64 oh8 16 "
              "x2 16 x1 16 x0 16 iotaS 128 ohI 512 ohA 512 oh 512 kX 512 inX 512 rs 256 mq 256 sc 256 alH 256 alL 256 thHb 256 thLb 256 "
-             "win 1024 mB 1024 mask 1024 m2 512 cm 512 ysb 512"),
+             "win 1024 mask 1024 m2 512 cm 512 ysb 512"),
     "bufU": ("uint16", 16, "a16 32 e16 384 c16 320 f16 64 l16 96"),
 }
 SCRATCH = {}
@@ -37,11 +37,14 @@ for _n, _c, _type in (("seenB", 4096, "bfloat16"), ("vecB", 4096, "bfloat16"), (
 for _j in range(8):
     SCRATCH["p%d" % _j] = ("psum", [128, 512], "float32")
     TILES["p%d" % _j] = ("p%d" % _j, 0, 512)
-BLOCKS = {"rq1": 16, "rq2": 32, "rr1": 16, "rr2": 32, "rsp": RW}
+GROUPS = ((0, 2), (2, 6))
+BLOCKS = {"rsp": RW}
+for _j, (_a, _b) in enumerate(GROUPS):
+    BLOCKS["rq%d" % _j] = BLOCKS["rr%d" % _j] = 8 * (_b - _a)
 for _n, _c in BLOCKS.items():
     SCRATCH[_n] = ("sbuf", [128, N, _c], "bfloat16" if _n == "rsp" else "int32")
 SEMAPHORES = ("sv ss sp sg d_sd d_rk d_thr d_ali d_seen d_vec d_tab0 d_tab1 d_tab2 d_tab3 d_y d_ch "
-              "l_be l_rq1 l_rq2 l_rsp r_be r_rq1 r_rq2 r_rsp").split()
+              "l_be l_rsp r_be r_rsp").split() + ["%s_rq%d" % (_n, _j) for _n in "lr" for _j in range(len(GROUPS))]
 
 
 def engine_plan(core, T, topo):
@@ -147,6 +150,9 @@ def rank_program(g, core, T, topo):
     def act(out, a):
         run("S", lambda o, i: S.activation(o, i, AF.Copy), out, [a])
 
+    def scaled(out, a, by):
+        run("S", lambda o, i, c: S.activation(o, i, AF.Copy, scale=c), out, [a, by])
+
     def iota(out, pattern, base, cm, exact=False):
         run("G", lambda o: g.iota(o, pattern, base, cm) if exact else
             g.iota(o, pattern, base, cm, allow_small_or_imprecise_dtypes=True), out, [])
@@ -206,8 +212,8 @@ def rank_program(g, core, T, topo):
         return "%s:%d:%d" % (name, w * i, w * i + w)
 
     landing(lambda r: at("beR", 4, r), "r_be")
-    landing(lambda r: block("rr1", r), "r_rq1")
-    landing(lambda r: block("rr2", r), "r_rq2")
+    for j in range(len(GROUPS)):
+        landing(lambda r: block("rr%d" % j, r), "r_rq%d" % j)
     landing(lambda r: at("rspR", RW, r), "r_rsp")
 
     dma("Y", "sdI:0:1", ext(T.sd), "d_sd")
@@ -216,7 +222,8 @@ def rank_program(g, core, T, topo):
     dma("Y", "aliI", ext(T.ali), "d_ali")
     dma("Y", "seenB", ext(T.seen), "d_seen")
 
-    for name, c in (("ones", 1.0), ("onesB", 1.0), ("selB", 0.0), ("rs", 1.0), ("be", 0.0), ("yc", 0.0), ("rs:0:256:32", 0.0), ("tabs", 0.0)):
+    for name, c in (("ones", 1.0), ("onesB", 1.0), ("selB", 0.0), ("selX", 0.0), ("rs", 1.0), ("be", 0.0), ("yc", 0.0),
+                    ("rs:0:256:32", 0.0), ("tabs", 0.0)):
         fill(name, c)
     step = 1597 * (TRY + 1)
     iota("ckN", [[step, 32]], -int(BIG), 0, True)
@@ -260,55 +267,48 @@ def rank_program(g, core, T, topo):
     tt("oSr", "oB", "*", "oB")
     cp("x1:0:1", "r1:0:1")
     ts("c3:0:1", "p16F:0:1", "==", 3.0)
+    ts("w1:0:1", "p16F:0:1", "<", 3.0)
+    scaled("selK", "selB", 0.0625)
+    scaled("selC", "selB", "c3:0:1")
+    scaled("selA", "selB", "w1:0:1")
     tt("oA0", "oSr", "+", "oL2")
-    ts("selK", "selB", "*", 0.0625)
     tt("x0:0:1", "r1:0:1", "-", "x1:0:1")
     ts("oA", "oA0", ">>", 6, "&", 4095)
-    ts("sel2", "selB:13:141", "*", "x2:0:1")
-    ts("sel1", "selB:14:142", "*", "x1:0:1")
+    for j in range(3):
+        ts("selX:%d:128:16" % j, "g9:0:8", "*", "x%d:0:1" % j)
     for w in range(N):
         ts(at("p0" if w < 4 else "t8", 32, w % 4), "oA", ">=", 512.0 * w, "*", at("dyS", 1, w))
     ts("oW", "oA", ">>", 9)
     tt("p1:0:64", "p0:0:64", "+", "t8:0:64")
     tt("t4", "p0:64:128", "+", "t8:64:128")
-    ts("sel0", "selB:15:143", "*", "x0:0:1")
     tt("p0:128:160", "p1:0:32", "+", "t4:0:32")
     tt("y2", "p1:32:64", "+", "t4:32:64")
     tt("yI", "p0:128:160", "+", "y2")
-    mms("p7", [("sel%d" % j, "oh") for j in range(3)] + [("selK:12:140", "kX")])
+    mms("p7", [("selX", "oh"), ("selK:12:140", "kX")])
     act("inX", "p7")
     ts("oTh", "yI", "&", 8191)
     ts("oD", "yI", ">>", 13)
     tt("oF", "oB", ">=", "oTh")
-    ts("w0:0:1", "p16F:0:1", "<", 2.0)
     tt("oFd", "oF", "*", "oD")
-    ts("w2:0:1", "p16F:0:1", "==", 2.0, "*", 8192.0)
     tt("own", "oFd", "+", "oW")
-    ts("w1:0:1", "p16F:0:1", "<", 3.0)
     for q in range(N):
         ts(at("mq", 32, q), "own", "==", float(q))
-    ts("selC", "selB", "*", "c3:0:1")
     run("V", V.tensor_tensor_scan, "sc", ["rs", "mq"], 0.0, A_.mult, A_.add)
     mms("p2:0:8", [("lt", "sc:31:256:32")])
     act("be:1:32:4", "sc:31:256:32")
-    ts("selA", "selB", "*", "w1:0:1")
-    tt("w4:0:1", "w0:0:1", "+", "w2:0:1")
     tt("be:0:32:4", "p2:0:8", "+", "qc")
-    ts("w3:0:1", "c3:0:1", "*", 2097152.0)
     for q in range(N):
         ts(at("p1", 32, q), at("sc", 32, q), "+", "be:%d:%d" % (4 * q, 4 * q + 1))
     tt("p0:0:128", "p1:0:128", "*", "mq:0:128")
     tt("b8", "p1:128:256", "*", "mq:128:256")
-    tt("wcol:0:1", "w4:0:1", "+", "w3:0:1")
     tt("p0:128:192", "p0:0:64", "+", "b8:0:64")
     tt("b4", "p0:64:128", "+", "b8:64:128")
-    ts("selT", "selB", "*", "wcol:0:1")
     tt("b2", "p0:128:192", "+", "b4")
     tt("v", "b2:0:32", "+", "b2:32:64")
     cp("a16", "v")
     send("r_be", lambda q: at("be", 4, q), at("beR", 4, me), "l_be")
     cp("win@a16", "inX")
-    for out, sel in (("p5:0:64", "selA"), ("p4:0:64", "selC")):
+    for out, sel in (("p4:0:64", "selC"), ("p5:0:64", "selA")):
         mms(out, [("%s:%d:%d" % (sel, 15 - b, 143 - b), "win:%d:1024:16" % b) for b in range(16)])
 
     cp("alH", "aliI")
@@ -334,13 +334,14 @@ def rank_program(g, core, T, topo):
         def other(k=1):
             for _ in range(k):
                 if m:
-                    ts(*m.pop(0))
+                    c = m.pop(0)
+                    c[0](*c[1:])
 
         def r(tile):
             return R(tile, i0, n)
 
         for i in range(i0, i1):
-            ts(R("kk", i), "p4:0:64", "*", float(step), "+", 1597.0 * (i + 1) - BIG)
+            run("S", lambda o, x: S.activation(o, x, AF.Copy, bias=1597.0 * (i + 1) - BIG, scale=float(step)), R("kk", i), ["p4:0:64"])
         if i0 == 0:
             cp("sT", "p5:0:64")
         for i in range(i0, i1):
@@ -348,9 +349,10 @@ def rank_program(g, core, T, topo):
         if i0 == 0:
             ts("hs", "sT", ">>", 12)
         ts(r("hL"), r("hT"), "&", 4095)
-        for i in range(i0, i1):
-            ts(R("H6", i), "hs", "*", 64.0, "+", -BIG)
-        q, rr, q0 = R("p6", 0, n), R("p6", 4, n), "p7:0:%d" % (64 * n)
+        if i0 == 0:
+            for i in range(i1):
+                ts(R("H6", i), "hs", "*", 64.0, "+", -BIG)
+        q, rr, q0 = R("p6", 0, n), R("p3", 0, n), "p7:0:%d" % (64 * n)
         tt(q, r("hL"), "*", r("hL"))
         ts(r("hL2"), r("hL"), "*", 64.0, "+", -BIG)
         tt(r("hb"), q, "+", r("H6"))
@@ -365,19 +367,33 @@ def rank_program(g, core, T, topo):
         other()
         for i in range(i0, i1):
             tt(parts("rq" + name, 8 * (i - i0), 8 * (i - i0) + 8), R("p7", i - i0), "+", R("hA", i))
+        if i0 == 0:
+            for i in range(i1, TRY):
+                act(R("H6", i), "H6:0:64")
         send("r_rq" + name, lambda q: block("rq" + name, q), block("rr" + name, me), "l_rq" + name)
         other(len(m))
         cp(block("rr" + name, me), block("rq" + name, me))
 
-    hashes(0, 2, "1", [])
-    hashes(2, TRY, "2", [("lo", "beR:0:32:4", "+", -float(128 * me - 1))] +
-           [(at("p0" if r < 4 else "p1", 128, r % 4), "iotaS", ">=", at("lo", 1, r), "*", float(2 ** (7 - r))) for r in range(N)])
-    tt("hi", "lo", "+", "beR:1:32:4")
+    spare = [(ts, "ha2", "beR:1:32:4", "*", 0.5, "+", -0.25), (ts, "nm0", "beR:1:32:4", "*", -0.5, "+", 0.5 + float(128 * me - 1)),
+             (tt, "nm", "nm0", "-", "beR:0:32:4")]
+    for j, (i0, i1) in enumerate(GROUPS):
+        hashes(i0, i1, str(j), spare if j == len(GROUPS) - 1 else [])
     for r in range(N):
-        ts(at("mB", 128, r), "iotaS", ">=", at("hi", 1, r), "*", float(2 ** (7 - r)))
+        run("S", lambda o, i, b: S.activation(o, i, AF.Abs, bias=b), at("mT", 128, r), ["iotaS", at("nm", 1, r)])
+
+    ts("w0:0:1", "p16F:0:1", "<", 2.0)
+    ts("w2:0:1", "p16F:0:1", "==", 2.0, "*", 8192.0)
+    ts("w3:0:1", "c3:0:1", "*", 2097152.0)
+    tt("w4:0:1", "w0:0:1", "+", "w2:0:1")
+    ts("w6:0:1", "p16F:0:1", "<", 8.0)
+    ts("w5:0:1", "p16F:0:1", ">=", 8.0)
+    tt("wcol:0:1", "w4:0:1", "+", "w3:0:1")
+    tt("oh8:0:8", "oh:0:8", "+", "oh:8:16")
 
     def packed(i):
-        return parts("rr1", 8 * i, 8 * i + 8) if i < 2 else parts("rr2", 8 * i - 16, 8 * i - 8)
+        for j, (i0, i1) in enumerate(GROUPS):
+            if i0 <= i < i1:
+                return parts("rr%d" % j, 8 * (i - i0), 8 * (i - i0) + 8)
 
     def places(i0, i1):
         for i in range(i0, i1):
@@ -402,46 +418,50 @@ def rank_program(g, core, T, topo):
         ops = [(tt, R("xI", i), bank(i) + ":0:64", "min", packed(i)), (ts, R("cI", i), R("xI", i), "&", 4095)]
         if i < TRY - 1:
             ops.append((cp, R("c16", i), R("cI", i)))
-        return ops + ([(tt, R("dI", i - 1), R("cI", i), "-", R("cI", i - 1))] if i else [])
+            ops.append((ts, R("kI", i), R("cI", i), "+", 4096.0 * (TRY - 1 - i)))
+        return ops
 
     def known(j):
-        return [(cp, R("wI", j), "p%d:0:64" % (3 + j % 3)), (ts, R("sI", j), R("wI", j), ">>", 7, "&", 1)]
+        return [(cp, R("wI", j), "p%d:0:64" % (3 + j % 3)), (ts, R("sI", j), R("wI", j), "&", 1 << 15)]
 
     def go(j):
-        p = R("pr", j) if j else R("sI", 0)
-        return ([(tt, p, R("pr" if j > 1 else "sI", j - 1), "*", R("sI", j))] if j else []) + \
-            [(tt, R("mI", j), p, "*", R("dI", j)), (tt, R("acc", j), R("acc", j - 1) if j else R("cI", 0), "+", R("mI", j))]
+        k = "p%d" % (j % 2)
+        if j == 0:
+            return [(tt, R("acc", 0), R("kI", 0), "-", R("sI", 0))]
+        return [(tt, k + ":0:64", R("kI", j), "-", R("sI", j)), (tt, R("acc", j), k + ":0:64", "max", R("acc", j - 1))]
 
-    places(0, 2)
+    places(*GROUPS[0])
     act("tg:0:512", "tabs@e16:0:32")
+    scaled("selT", "selB", "wcol:0:1")
     cp("tg:512:1024", "tabs@e16:32:64")
     table(0)
-    act("tg:1024:2048", "tabs@" + R("e16", 1))
+    act(at("tg", 1024, 1), "tabs@" + R("e16", 1))
+    for r in range(N):
+        ts(at("mask", 128, r), at("mT", 128, r), "<", at("ha2", 1, r), "*", float(2 ** (15 - r)))
     table(1)
-    tt("mask:0:512", "p0", "-", "mB:0:512")
-    tt("mask:512:1024", "p1", "-", "mB:512:1024")
     weave(item(0))
     seen(0)
-    places(2, TRY)
-    for i in range(2, TRY):
+    places(*GROUPS[1])
+    for i in range(*GROUPS[1]):
         act(at("tg", 1024, i), "tabs@" + R("e16", i))
     table(2)
     weave(item(1))
     seen(1)
-    ts("w6:0:1", "p16F:0:1", "<", 8.0)
-    ts("w5:0:1", "p16F:0:1", ">=", 8.0)
     for out, a, c in (("wI0", "idn", "w6"), ("wU", "up8", "w6"), ("wI1", "idn", "w5"), ("wD", "dn8", "w5")):
-        ts(out, a, "*", c + ":0:1")
-    tt("oh8:0:8", "oh:0:8", "+", "oh:8:16")
+        scaled(out, a, c + ":0:1")
     for i in range(2, TRY - 1):
         table(i + 1)
         weave(go(i - 3) if i > 2 else [], item(i), known(i - 2))
         seen(i)
     weave(go(2), item(5), known(3))
-    last = go(3)
-    weave(last[:2] + [(tt, "qI", R("pr", 3), "*", R("dI", 4)), (cp, R("wI", 4), "p4:0:64"), last[2], known(4)[1]])
-    tt(R("mI", 4), R("sI", 4), "*", "qI")
-    tt(R("acc", 4), R("acc", 3), "+", R("mI", 4))
+    weave(go(3)[:1])
+    cp(R("wI", 4), "p4:0:64")
+    tt(R("acc", 3), "p1:0:64", "max", R("acc", 2))
+    ts(R("sI", 4), R("wI", 4), "&", 1 << 15)
+    tt("a6", R("acc", 3), "max", R("cI", 5))
+    tt("p0:0:64", R("kI", 4), "-", R("sI", 4))
+    tt("aA", "p0:0:64", "max", "a6")
+    ts(R("acc", 4), "aA", "&", 4095)
     cp("f16", R("acc", 4))
 
     def features(q, r):
@@ -449,19 +469,19 @@ def rank_program(g, core, T, topo):
         (act if q == "S" else cp)(out, "vecB@" + at("f16", 8, r))
 
     order = [T.rank_of(c) for c in off + on] + [me]
-    features("S", order[0])
     cp("iH", R("acc", 4))
+    features("S", order[0])
+    features("V", order[2])
     features("S", order[1])
-    features("S", order[2])
-    features("V", order[3])
     tt("iL", R("acc", 4), "-", "iH")
+    features("V", order[3])
     mms("p2:0:64", [("wU", "iH"), ("wI0", "iL")])
     mms("p2:64:128", [("wD", "iH"), ("wI1", "iL")])
     features("S", order[4])
     features("V", order[5])
+    features("S", order[6])
     for h in range(2):
         cp(parts("rsp", 128 + 8 * h, 136 + 8 * h), "p2:%d:%d" % (64 * h, 64 * h + 64))
-    features("S", order[6])
     send("r_rsp", lambda q: block("rsp", q), at("rspR", RW, me), "l_rsp")
     features("V", order[7])
     cp("rspR:%d:%d" % (RW * me + 128, RW * me + RW), block("rsp", me, 128, RW))

@@ -9,17 +9,17 @@ OPS = {"+": A_.add, "-": A_.subtract, "*": A_.mult, "min": A_.min, "max": A_.max
        "==": A_.is_equal, ">>": A_.arith_shift_right, "&": A_.bitwise_and}
 
 SMALL = {
-    "bufI": ("int32", 8, "ckN 32 pI 8 p16I 8 sdI 8 hI 8 rkI 16 oT 32 oL 32 oL2 32 oSq 32 oB0 32 oB 32 oSr 32 oA0 32 oA 32 oW 32 yI 32 "
-             "oTh 32 oD 32 v 32 thrI 256 aliI 256 thH 256 thL 256 sT 64 hs 64 hT 384 hL 384 hL2 384 "
+    "bufI": ("int32", 8, "ckN 32 pI 8 p16I 8 sdI 8 hI 8 lI 8 ckp 8 ckA 8 rkI 16 oT 32 oL 32 oL2 32 oSq 32 oB0 32 oB 32 oSr 32 oA0 32 oA 32 "
+             "oW 32 yI 256 oTh 32 oD 32 v 32 thrI 256 aliI 256 thH 256 thL 256 hT 384 hL 384 "
              "hb 384 hB 384 ha 384 hA 384 eI 384 xI 384 cI 384 kI 320 wI 320 sI 320 acc 320 a6 64 aA 64 q1 32 "
              "q16 32 ps 32 mm 32 cq 32 cl 32 bl 32 b8I 32 mb 32"),
     "bufF": ("float32", 8, "ones 128 p16F 8 n16 8 e8a 128 e8 128 wc 8 g9a 16 g9 16 qc 8 w0 8 w1 8 w2 8 w3 8 w4 8 w5 8 w6 8 wcol 8 c3 8 "
-             "ya 8 yb 8 yc 16 dy 8 dyS 8 sF 8 hF 8 r1 8 t8 128 t4 64 oF 32 oFd 32 own 32 be 32 beR 32 b8 128 b4 64 "
-             "b2 64 y2 32 kk 384 H6 384 ha2 8 nm 8 nm0 8 mT 1024 q4k 32 ch1 32"),
-    "bufB": ("bfloat16", 16, "onesB 128 lta 128 lt 128 selB 144 selT 144 selA 144 selC 144 selK 144 selX 128 "
+             "ya 8 yb 8 yc 16 dy 8 dyS 8 sF 8 hF 8 st 256 mqF 256 oF 32 oFd 32 own 32 be 32 beR 32 b8 128 b4 64 "
+             "b2 64 hL2 384 H6 384 ha2 8 nm 8 nm0 8 mT 1024 q4k 32 ch1 32"),
+    "bufB": ("bfloat16", 16, "onesB 128 ones5 512 lta 128 lt 128 selB 144 selT 144 selA 144 selC 144 selX 128 ckL 128 "
              "idn 128 up8 128 dn8 128 wI0 128 wI1 128 wU 128 wD 128 iH 64 iL 64 oh8 16 "
-             "x2 16 x1 16 x0 16 iotaS 128 ohI 512 ohA 512 oh 512 kX 512 inX 512 rs 256 mq 256 sc 256 alH 256 alL 256 thHb 256 thLb 256 "
-             "win 1024 mask 1024 m2 512 cm 512 ysb 512"),
+             "l1 16 l0 16 h1 16 h0 16 c1 16 c0 16 iotaS 128 ohI 512 ohA 512 oh 512 kE 512 inX 512 rs 256 rsw 256 mq 256 sc 256 "
+             "alH 256 alL 256 thHb 256 thLb 256 win 1024 mask 1024 m2 512 cm 512 ysb 512"),
     "bufU": ("uint16", 16, "a16 32 e16 384 c16 320 f16 64 l16 96"),
 }
 SCRATCH = {}
@@ -141,14 +141,25 @@ def rank_program(g, core, T, topo):
     def fill(out, c):
         run("V", V.memset, out, [], c)
 
+    def scan(out, a, b):
+        run("V", V.tensor_tensor_scan, out, [a, b], 0.0, A_.mult, A_.add)
+
+    idle = []
+
+    def gap(k=1):
+        for _ in range(k):
+            if idle:
+                c = idle.pop(0)
+                c[0](*c[1:])
+
     def weave(*chains):
         for j in range(max(len(c) for c in chains)):
             for c in chains:
                 if j < len(c):
                     c[j][0](*c[j][1:])
 
-    def act(out, a):
-        run("S", lambda o, i: S.activation(o, i, AF.Copy), out, [a])
+    def act(out, a, bias=0.0, scale=1.0):
+        run("S", lambda o, i: S.activation(o, i, AF.Copy, bias=bias, scale=scale), out, [a])
 
     def scaled(out, a, by):
         run("S", lambda o, i, c: S.activation(o, i, AF.Copy, scale=c), out, [a, by])
@@ -222,25 +233,35 @@ def rank_program(g, core, T, topo):
     dma("Y", "aliI", ext(T.ali), "d_ali")
     dma("Y", "seenB", ext(T.seen), "d_seen")
 
-    for name, c in (("ones", 1.0), ("onesB", 1.0), ("selB", 0.0), ("selX", 0.0), ("rs", 1.0), ("be", 0.0), ("yc", 0.0),
-                    ("rs:0:256:32", 0.0), ("tabs", 0.0)):
+    for name, c in (("ones", 1.0), ("onesB", 1.0), ("ones5", 1.0), ("selB", 0.0), ("selX", 0.0), ("ckL", 0.0), ("win", 0.0),
+                    ("yc", 0.0), ("be", 0.0), ("rs", 1.0)):
         fill(name, c)
     step = 1597 * (TRY + 1)
     iota("ckN", [[step, 32]], -int(BIG), 0, True)
-    iota("8|wc", [[-8192, 8]], 0, 0)
     iota("pI:0:1", [[0, 1]], 0, 1, True)
+    iota("8|wc", [[-8192, 8]], 0, 0)
     keep("8|e8a", "8|ones", [[1, 128]], ">=", 0, -16)
-    keep("g9a:0:9", "ones:0:9", [[-16, 9]], ">=", 0, 1)
     keep("8|e8", "8|e8a", [[-1, 128]], ">=", 15, 16)
+    keep("g9a:0:9", "ones:0:9", [[-16, 9]], ">=", 0, 1)
     keep("g9:0:9", "g9a:0:9", [[16, 9]], ">=", 15, -1)
     iota("ohI", [[0, 32], [1, 16]], 0, 0)
+    iota("ckp:0:1", [[0, 1]], 0, step, True)
     keep("lta", "onesB", [[16, 8], [1, 16]], ">", 0, -1)
     keep("lt", "lta", [[-16, 8], [0, 16]], ">=", 0, 1)
     iota("qc", [[128, 8]], -1, 0)
-    iota("kX", [[1, 32], [0, 16]], 0, 0)
-    iota("win", [[0, 1024]], 0, 0)
+    keep("kE", "ones5", [[1, 32], [0, 16]], "==", 0, -1)
     iota("iotaS", [[1, 128]], 0, 0)
+    ts("p16I:0:1", "pI:0:1", "&", 15)
+    fill("rs:0:256:32", 0.0)
+    cp("p16F:0:1", "p16I:0:1")
+    ts("n16:0:1", "p16F:0:1", "*", -1.0)
+    act("tabs:0:1024", "win")
 
+    idle += [(ts, "w1:0:1", "p16F:0:1", "<", 4.0), (ts, "c3:0:1", "p16F:0:1", ">=", 4.0),
+             (ts, "w0:0:1", "p16F:0:1", "<", 2.0), (ts, "w2:0:1", "p16F:0:1", "==", 2.0, "*", 8192.0),
+             (ts, "w3:0:1", "p16F:0:1", "==", 3.0, "*", 2097152.0), (tt, "w4:0:1", "w0:0:1", "+", "w2:0:1"),
+             (ts, "w6:0:1", "p16F:0:1", "<", 8.0), (tt, "wcol:0:1", "w4:0:1", "+", "w3:0:1"), (ts, "w5:0:1", "p16F:0:1", ">=", 8.0),
+             (tt, "oh8:0:8", "oh:0:8", "+", "oh:8:16")]
     cp("sF:0:1", "sdI:0:1")
     ts("hI:0:1", "sdI:0:1", ">>", 12)
     ts("8|ya", "8|rkI:8:16", "*", 8192.0)
@@ -248,67 +269,78 @@ def rank_program(g, core, T, topo):
     ts("hF:0:1", "hI:0:1", "*", 64.0, "+", -BIG)
     tt("8|yb", "8|ya", "+", "8|wc")
     ts("oL", "oT", "&", 4095)
-    cp("x2:0:1", "sF:0:1")
+    ts("lI:0:1", "sdI:0:1", "&", 4095)
     tt("8|yc:1:9", "8|yb", "+", "8|rkI:0:8")
     tt("oSq", "oL", "*", "oL")
-    ts("p16I:0:1", "pI:0:1", "&", 15)
+    cp("l1:0:1", "lI:0:1")
     tt("8|dy", "8|yc:1:9", "-", "8|yc:0:8")
     ts("oB0", "oSq", "+", "hF:0:1")
     mms("p3:0:8", [("8|e8", "8|dy")])
     act("dyS", "p3:0:8")
-    ts("oL2", "oL", "*", 64.0, "+", -BIG)
-    cp("p16F:0:1", "p16I:0:1")
+    cp("h1:0:1", "hI:0:1")
+    fill("rsw", 1.0)
     ts("oB", "oB0", ">>", 6, "&", 4095)
-    ts("n16:0:1", "p16F:0:1", "*", -1.0)
+    ts("oL2", "oL", "*", 64.0, "+", -BIG)
     run("S", lambda o, i, b: S.activation(o, i, AF.Abs, bias=b), "ohA", ["ohI", "n16:0:1"])
     run("S", lambda o, i: S.activation(o, i, AF.Relu, bias=1.0, scale=-1.0), "oh", ["ohA"])
-    tt("r1:0:1", "sF:0:1", "-", "x2:0:1")
-    cp("selB:15:144:16", "g9:0:9")
     tt("oSr", "oB", "*", "oB")
-    cp("x1:0:1", "r1:0:1")
-    ts("c3:0:1", "p16F:0:1", "==", 3.0)
-    ts("w1:0:1", "p16F:0:1", "<", 3.0)
-    scaled("selK", "selB", 0.0625)
-    scaled("selC", "selB", "c3:0:1")
-    scaled("selA", "selB", "w1:0:1")
+    tt("l0:0:1", "lI:0:1", "-", "l1:0:1")
     tt("oA0", "oSr", "+", "oL2")
-    tt("x0:0:1", "r1:0:1", "-", "x1:0:1")
+    fill("rsw:0:256:8", 0.0)
+    tt("h0:0:1", "hI:0:1", "-", "h1:0:1")
     ts("oA", "oA0", ">>", 6, "&", 4095)
-    for j in range(3):
-        ts("selX:%d:128:16" % j, "g9:0:8", "*", "x%d:0:1" % j)
+    ts("selX:0:128:16", "g9:0:8", "*", "l1:0:1")
     for w in range(N):
-        ts(at("p0" if w < 4 else "t8", 32, w % 4), "oA", ">=", 512.0 * w, "*", at("dyS", 1, w))
+        ts("st:%d:256:8" % w, "oA", ">=", 512.0 * w, "*", at("dyS", 1, w))
     ts("oW", "oA", ">>", 9)
-    tt("p1:0:64", "p0:0:64", "+", "t8:0:64")
-    tt("t4", "p0:64:128", "+", "t8:64:128")
-    tt("p0:128:160", "p1:0:32", "+", "t4:0:32")
-    tt("y2", "p1:32:64", "+", "t4:32:64")
-    tt("yI", "p0:128:160", "+", "y2")
-    mms("p7", [("selX", "oh"), ("selK:12:140", "kX")])
-    act("inX", "p7")
-    ts("oTh", "yI", "&", 8191)
-    ts("oD", "yI", ">>", 13)
+    scan("yI", "rsw", "st")
+    ts("selX:1:128:16", "g9:0:8", "*", "l0:0:1")
+    ts("selX:4:128:16", "g9:0:8", "*", "h1:0:1")
+    ts("oTh", "yI:7:256:8", "&", 8191)
+    ts("oD", "yI:7:256:8", ">>", 13)
+    ts("selX:5:128:16", "g9:0:8", "*", "h0:0:1")
     tt("oF", "oB", ">=", "oTh")
+    ts("ckA:0:1", "ckp:0:1", "&", 4095)
     tt("oFd", "oF", "*", "oD")
+    cp("c1:0:1", "ckA:0:1")
     tt("own", "oFd", "+", "oW")
+    cp("selB:15:144:16", "g9:0:9")
     for q in range(N):
         ts(at("mq", 32, q), "own", "==", float(q))
-    run("V", V.tensor_tensor_scan, "sc", ["rs", "mq"], 0.0, A_.mult, A_.add)
+    tt("c0:0:1", "ckA:0:1", "-", "c1:0:1")
+    ts("ckL:2:128:16", "onesB:0:8", "*", "c1:0:1")
+    scan("sc", "rs", "mq")
+    ts("ckL:3:128:16", "onesB:0:8", "*", "c0:0:1")
     mms("p2:0:8", [("lt", "sc:31:256:32")])
+    mms("p7", [("selX", "oh"), ("ckL", "kE")])
     act("be:1:32:4", "sc:31:256:32")
+    cp("mqF", "mq")
     tt("be:0:32:4", "p2:0:8", "+", "qc")
-    for q in range(N):
-        ts(at("p1", 32, q), at("sc", 32, q), "+", "be:%d:%d" % (4 * q, 4 * q + 1))
+    act("inX", "p7")
+    gap()
+    tt("mqF:0:256:32", "mq:0:256:32", "+", "be:0:32:4")
+    gap()
+    scan("p1:0:256", "rs", "mqF")
+    gap()
     tt("p0:0:128", "p1:0:128", "*", "mq:0:128")
     tt("b8", "p1:128:256", "*", "mq:128:256")
+    gap()
     tt("p0:128:192", "p0:0:64", "+", "b8:0:64")
     tt("b4", "p0:64:128", "+", "b8:64:128")
+    gap()
     tt("b2", "p0:128:192", "+", "b4")
+    gap()
     tt("v", "b2:0:32", "+", "b2:32:64")
+    gap()
     cp("a16", "v")
+    gap()
     send("r_be", lambda q: at("be", 4, q), at("beR", 4, me), "l_be")
+    scaled("selA", "selB", "w1:0:1")
+    scaled("selC", "selB", "c3:0:1")
+    act("tabs:1024:2048", "tabs:0:1024")
+    act("tabs:2048:4096", "tabs:0:2048")
     cp("win@a16", "inX")
-    for out, sel in (("p4:0:64", "selC"), ("p5:0:64", "selA")):
+    for out, sel in (("p4:0:64", "selA"), ("p5:0:64", "selC")):
         mms(out, [("%s:%d:%d" % (sel, 15 - b, 143 - b), "win:%d:1024:16" % b) for b in range(16)])
 
     cp("alH", "aliI")
@@ -328,67 +360,53 @@ def rank_program(g, core, T, topo):
     def R(name, i, n=1):
         return "%s:%d:%d" % (name, 64 * i, 64 * i + 64 * n)
 
-    def hashes(i0, i1, name, beside):
-        n, m = i1 - i0, list(beside)
+    def counter(i):
+        return float(1597 * (i + 1) % 4096)
 
-        def other(k=1):
-            for _ in range(k):
-                if m:
-                    c = m.pop(0)
-                    c[0](*c[1:])
+    def hashes(i0, i1, name):
+        n = i1 - i0
 
         def r(tile):
             return R(tile, i0, n)
 
         for i in range(i0, i1):
-            run("S", lambda o, x: S.activation(o, x, AF.Copy, bias=1597.0 * (i + 1) - BIG, scale=float(step)), R("kk", i), ["p4:0:64"])
-        if i0 == 0:
-            cp("sT", "p5:0:64")
-        for i in range(i0, i1):
-            tt(R("hT", i), "p5:0:64", "+", R("kk", i))
-        if i0 == 0:
-            ts("hs", "sT", ">>", 12)
-        ts(r("hL"), r("hT"), "&", 4095)
+            act(R("H6", i), "p5:0:64", -BIG, 64.0)
         if i0 == 0:
             for i in range(i1):
-                ts(R("H6", i), "hs", "*", 64.0, "+", -BIG)
+                ts(R("hT", i), "p4:0:64", "+", counter(i))
+        ts(r("hL"), r("hT"), "&", 4095)
+        if i0 == 0:
+            for i in range(i1, TRY):
+                ts(R("hT", i), "p4:0:64", "+", counter(i))
+        for i in range(i0, i1):
+            act(R("hL2", i), "p4:0:64", 64.0 * counter(i) - BIG, 64.0)
         q, rr, q0 = R("p6", 0, n), R("p3", 0, n), "p7:0:%d" % (64 * n)
+        gap()
         tt(q, r("hL"), "*", r("hL"))
-        ts(r("hL2"), r("hL"), "*", 64.0, "+", -BIG)
+        gap()
         tt(r("hb"), q, "+", r("H6"))
-        other()
+        gap()
         ts(r("hB"), r("hb"), ">>", 6, "&", 4095)
-        other()
+        gap()
         tt(rr, r("hB"), "*", r("hB"))
         ts(q0, r("hB"), "*", 8192.0, "+", 4096.0 - 16777216.0)
         tt(r("ha"), rr, "+", r("hL2"))
-        other()
+        gap()
         ts(r("hA"), r("ha"), ">>", 6, "&", 4095)
-        other()
+        gap()
         for i in range(i0, i1):
             tt(parts("rq" + name, 8 * (i - i0), 8 * (i - i0) + 8), R("p7", i - i0), "+", R("hA", i))
-        if i0 == 0:
-            for i in range(i1, TRY):
-                act(R("H6", i), "H6:0:64")
         send("r_rq" + name, lambda q: block("rq" + name, q), block("rr" + name, me), "l_rq" + name)
-        other(len(m))
-        cp(block("rr" + name, me), block("rq" + name, me))
+        idle.insert(0, (cp, block("rr" + name, me), block("rq" + name, me)))
 
-    spare = [(ts, "ha2", "beR:1:32:4", "*", 0.5, "+", -0.25), (ts, "nm0", "beR:1:32:4", "*", -0.5, "+", 0.5 + float(128 * me - 1)),
-             (tt, "nm", "nm0", "-", "beR:0:32:4")]
-    for j, (i0, i1) in enumerate(GROUPS):
-        hashes(i0, i1, str(j), spare if j == len(GROUPS) - 1 else [])
+    hashes(*GROUPS[0], "0")
+    idle += [(ts, "ha2", "beR:1:32:4", "*", 0.5, "+", -0.25),
+             (ts, "nm0", "beR:1:32:4", "*", -0.5, "+", 0.5 + float(128 * me - 1)), (tt, "nm", "nm0", "-", "beR:0:32:4")]
+    hashes(*GROUPS[1], "1")
+    own1 = idle.pop(0)
+    gap(len(idle))
     for r in range(N):
         run("S", lambda o, i, b: S.activation(o, i, AF.Abs, bias=b), at("mT", 128, r), ["iotaS", at("nm", 1, r)])
-
-    ts("w0:0:1", "p16F:0:1", "<", 2.0)
-    ts("w2:0:1", "p16F:0:1", "==", 2.0, "*", 8192.0)
-    ts("w3:0:1", "c3:0:1", "*", 2097152.0)
-    tt("w4:0:1", "w0:0:1", "+", "w2:0:1")
-    ts("w6:0:1", "p16F:0:1", "<", 8.0)
-    ts("w5:0:1", "p16F:0:1", ">=", 8.0)
-    tt("wcol:0:1", "w4:0:1", "+", "w3:0:1")
-    tt("oh8:0:8", "oh:0:8", "+", "oh:8:16")
 
     def packed(i):
         for j, (i0, i1) in enumerate(GROUPS):
@@ -396,10 +414,7 @@ def rank_program(g, core, T, topo):
                 return parts("rr%d" % j, 8 * (i - i0), 8 * (i - i0) + 8)
 
     def places(i0, i1):
-        for i in range(i0, i1):
-            ts(R("eI", i), packed(i), "&", 4095)
-        for i in range(i0, i1):
-            cp(R("e16", i), R("eI", i))
+        return [(ts, R("eI", i), packed(i), "&", 4095) for i in range(i0, i1)] + [(cp, R("e16", i), R("eI", i)) for i in range(i0, i1)]
 
     def wrap(out, sel, src, i):
         mms(out + ":0:64", [("%s:%d:%d" % (sel, 15 - b, 143 - b), "%s:%d:%d:16" % (src, 1024 * i + b, 1024 * i + 1024)) for b in range(16)])
@@ -430,22 +445,27 @@ def rank_program(g, core, T, topo):
             return [(tt, R("acc", 0), R("kI", 0), "-", R("sI", 0))]
         return [(tt, k + ":0:64", R("kI", j), "-", R("sI", j)), (tt, R("acc", j), k + ":0:64", "max", R("acc", j - 1))]
 
-    places(*GROUPS[0])
+    weave(places(*GROUPS[0]))
     act("tg:0:512", "tabs@e16:0:32")
     scaled("selT", "selB", "wcol:0:1")
     cp("tg:512:1024", "tabs@e16:32:64")
     table(0)
     act(at("tg", 1024, 1), "tabs@" + R("e16", 1))
+    own1[0](*own1[1:])
     for r in range(N):
         ts(at("mask", 128, r), at("mT", 128, r), "<", at("ha2", 1, r), "*", float(2 ** (15 - r)))
     table(1)
     weave(item(0))
     seen(0)
-    places(*GROUPS[1])
-    for i in range(*GROUPS[1]):
+    late = places(*GROUPS[1])
+    weave(late[0:4] + late[4:6])
+    for i in (2, 3):
+        act(at("tg", 1024, i), "tabs@" + R("e16", i))
+    weave(item(1)[0:2], late[6:8])
+    weave(item(1)[2:])
+    for i in (4, 5):
         act(at("tg", 1024, i), "tabs@" + R("e16", i))
     table(2)
-    weave(item(1))
     seen(1)
     for out, a, c in (("wI0", "idn", "w6"), ("wU", "up8", "w6"), ("wI1", "idn", "w5"), ("wD", "dn8", "w5")):
         scaled(out, a, c + ":0:1")

@@ -9,17 +9,17 @@ OPS = {"+": A_.add, "-": A_.subtract, "*": A_.mult, "min": A_.min, "max": A_.max
        "==": A_.is_equal, ">>": A_.arith_shift_right, "&": A_.bitwise_and}
 
 SMALL = {
-    "bufI": ("int32", 8, "ckN 32 pI 8 p16I 8 sdI 8 hI 8 lI 8 ckp 8 ckA 8 rkI 16 oT 32 oL 32 oL2 32 oSq 32 oB0 32 oB 32 oSr 32 oA0 32 oA 32 "
-             "oW 32 yI 256 oTh 32 oD 32 v 32 thrI 256 aliI 256 thH 256 thL 256 hT 384 hL 384 "
-             "hb 384 hB 384 ha 384 hA 384 eI 384 xI 384 cI 384 kI 320 wI 320 sI 320 acc 320 a6 64 aA 64 q1 32 "
+    "bufI": ("int32", 8, "ckN 32 pI 8 p16I 8 sdI 8 hI 8 lh 8 ckp 8 ckA 8 rkI 16 oT 32 oL 32 oL2 32 oSq 32 oB0 32 oB 32 oSr 32 oA0 32 oA 32 "
+             "oW 32 oB16 32 oP 32 oM 32 own 32 yI 256 v1 32 v 32 thrI 256 aliI 256 xl 64 xh 64 hT 384 hL 384 "
+             "hb 384 hB 384 ha 384 hA 384 pk 384 xI 384 cI 384 wI 320 sI 320 acc 320 a6 64 aA 64 r 64 wL 64 sL 64 q1 32 "
              "q16 32 ps 32 mm 32 cq 32 cl 32 bl 32 b8I 32 mb 32"),
-    "bufF": ("float32", 8, "ones 128 p16F 8 n16 8 e8a 128 e8 128 wc 8 g9a 16 g9 16 qc 8 w0 8 w1 8 w2 8 w3 8 w4 8 w5 8 w6 8 wcol 8 c3 8 "
-             "ya 8 yb 8 yc 16 dy 8 dyS 8 sF 8 hF 8 st 256 mqF 256 oF 32 oFd 32 own 32 be 32 beR 32 b8 128 b4 64 "
-             "b2 64 hL2 384 H6 384 ha2 8 nm 8 nm0 8 mT 1024 q4k 32 ch1 32"),
-    "bufB": ("bfloat16", 16, "onesB 128 ones5 512 lta 128 lt 128 selB 144 selT 144 selA 144 selC 144 selX 128 ckL 128 "
-             "idn 128 up8 128 dn8 128 wI0 128 wI1 128 wU 128 wD 128 iH 64 iL 64 oh8 16 "
-             "l1 16 l0 16 h1 16 h0 16 c1 16 c0 16 iotaS 128 ohI 512 ohA 512 oh 512 kE 512 inX 512 rs 256 rsw 256 mq 256 sc 256 "
-             "alH 256 alL 256 thHb 256 thLb 256 win 1024 mask 1024 m2 512 cm 512 ysb 512"),
+    "bufF": ("float32", 8, "ones 128 p16F 8 n16 8 e8a 128 e8 128 g9a 16 g9 16 w2 8 w5 8 w6 8 wcol 8 c3 8 wS 8 lhF 8 ckF 8 "
+             "ya 8 yc 16 dy 8 dyS 8 sF 8 hF 8 st 256 mqF 256 be 32 beR 32 b8 128 b4 64 "
+             "b2 64 xlF 64 H6 64 hL2 384 ha2 8 nm 8 nm0 8 mT 1024 q4k 32 ch1 32"),
+    "bufB": ("bfloat16", 16, "onesB 128 ones5 512 lta 128 lt 128 selB 144 selT 144 selP 144 selX 128 ckL 128 "
+             "idn 128 up8 128 dn8 128 wI0 128 wI1 128 wU 128 wD 128 iH 64 iL 64 oh8 16 q8 16 "
+             "iotaS 128 ohI 512 ohA 512 oh 512 kE 512 inX 512 rs 256 rsw 256 mq 256 sc 256 "
+             "alH 256 alL 256 thH 256 thL 256 win 1024 mask 1024 m2 512 cm 512 ysb 512"),
     "bufU": ("uint16", 16, "a16 32 e16 384 c16 320 f16 64 l16 96"),
 }
 SCRATCH = {}
@@ -31,20 +31,17 @@ for _buf, (_type, _step, _list) in SMALL.items():
         _at += -(-int(_c) // _step) * _step
     SCRATCH[_buf] = ("sbuf", [128, _at], _type)
 for _n, _c, _type in (("seenB", 4096, "bfloat16"), ("vecB", 4096, "bfloat16"), ("tabs", 4096, "bfloat16"),
-                      ("tg", 6144, "bfloat16"), ("sg", 5120, "bfloat16"), ("rspR", N * RW, "bfloat16")):
+                      ("tg", 6144, "bfloat16"), ("sg", 5120, "bfloat16"), ("su", 1024, "bfloat16"), ("rspR", N * RW, "bfloat16")):
     SCRATCH[_n] = ("sbuf", [128, _c], _type)
     TILES[_n] = (_n, 0, _c)
 for _j in range(8):
     SCRATCH["p%d" % _j] = ("psum", [128, 512], "float32")
     TILES["p%d" % _j] = ("p%d" % _j, 0, 512)
-GROUPS = ((0, 2), (2, 6))
-BLOCKS = {"rsp": RW}
-for _j, (_a, _b) in enumerate(GROUPS):
-    BLOCKS["rq%d" % _j] = BLOCKS["rr%d" % _j] = 8 * (_b - _a)
+BLOCKS = {"rsp": RW, "rq": 8, "rr": 8}
 for _n, _c in BLOCKS.items():
     SCRATCH[_n] = ("sbuf", [128, N, _c], "bfloat16" if _n == "rsp" else "int32")
 SEMAPHORES = ("sv ss sp sg d_sd d_rk d_thr d_ali d_seen d_vec d_tab0 d_tab1 d_tab2 d_tab3 d_y d_ch "
-              "l_be l_rsp r_be r_rsp").split() + ["%s_rq%d" % (_n, _j) for _n in "lr" for _j in range(len(GROUPS))]
+              "l_be l_rq l_rsp r_be r_rq r_rsp").split()
 
 
 def engine_plan(core, T, topo):
@@ -155,11 +152,11 @@ def rank_program(g, core, T, topo):
     def weave(*chains):
         for j in range(max(len(c) for c in chains)):
             for c in chains:
-                if j < len(c):
+                if j < len(c) and c[j]:
                     c[j][0](*c[j][1:])
 
-    def act(out, a, bias=0.0, scale=1.0):
-        run("S", lambda o, i: S.activation(o, i, AF.Copy, bias=bias, scale=scale), out, [a])
+    def act(out, a, bias=0.0, scale=1.0, func=AF.Copy):
+        run("S", lambda o, i: S.activation(o, i, func, bias=bias, scale=scale), out, [a])
 
     def scaled(out, a, by):
         run("S", lambda o, i, c: S.activation(o, i, AF.Copy, scale=c), out, [a, by])
@@ -187,9 +184,9 @@ def rank_program(g, core, T, topo):
 
     plan, off, on = engine_plan(core, T, topo)
 
-    def send(sem, src, dst, local):
+    def send(sem, src, dst, local, cores=None):
         tr = []
-        for c in off + on:
+        for c in cores or off + on:
             rid, pnc, _s = topo.addr(c)
             a, r = X(src(T.rank_of(c)))
             need("G", r, [])
@@ -223,8 +220,7 @@ def rank_program(g, core, T, topo):
         return "%s:%d:%d" % (name, w * i, w * i + w)
 
     landing(lambda r: at("beR", 4, r), "r_be")
-    for j in range(len(GROUPS)):
-        landing(lambda r: block("rr%d" % j, r), "r_rq%d" % j)
+    landing(lambda r: block("rr", r), "r_rq")
     landing(lambda r: at("rspR", RW, r), "r_rsp")
 
     dma("Y", "sdI:0:1", ext(T.sd), "d_sd")
@@ -233,22 +229,21 @@ def rank_program(g, core, T, topo):
     dma("Y", "aliI", ext(T.ali), "d_ali")
     dma("Y", "seenB", ext(T.seen), "d_seen")
 
-    for name, c in (("ones", 1.0), ("onesB", 1.0), ("ones5", 1.0), ("selB", 0.0), ("selX", 0.0), ("ckL", 0.0), ("win", 0.0),
+    for name, c in (("ones", 1.0), ("win", 0.0), ("onesB", 1.0), ("ones5", 1.0), ("selB", 0.0), ("selX", 0.0), ("ckL", 0.0),
                     ("yc", 0.0), ("be", 0.0), ("rs", 1.0)):
         fill(name, c)
     step = 1597 * (TRY + 1)
     iota("ckN", [[step, 32]], -int(BIG), 0, True)
     iota("pI:0:1", [[0, 1]], 0, 1, True)
-    iota("8|wc", [[-8192, 8]], 0, 0)
+    iota("ckp:0:1", [[0, 1]], 0, step, True)
+    iota("q8:0:8", [[1, 8]], 0, 0)
     keep("8|e8a", "8|ones", [[1, 128]], ">=", 0, -16)
     keep("8|e8", "8|e8a", [[-1, 128]], ">=", 15, 16)
     keep("g9a:0:9", "ones:0:9", [[-16, 9]], ">=", 0, 1)
     keep("g9:0:9", "g9a:0:9", [[16, 9]], ">=", 15, -1)
     iota("ohI", [[0, 32], [1, 16]], 0, 0)
-    iota("ckp:0:1", [[0, 1]], 0, step, True)
     keep("lta", "onesB", [[16, 8], [1, 16]], ">", 0, -1)
     keep("lt", "lta", [[-16, 8], [0, 16]], ">=", 0, 1)
-    iota("qc", [[128, 8]], -1, 0)
     keep("kE", "ones5", [[1, 32], [0, 16]], "==", 0, -1)
     iota("iotaS", [[1, 128]], 0, 0)
     ts("p16I:0:1", "pI:0:1", "&", 15)
@@ -256,69 +251,69 @@ def rank_program(g, core, T, topo):
     cp("p16F:0:1", "p16I:0:1")
     ts("n16:0:1", "p16F:0:1", "*", -1.0)
     act("tabs:0:1024", "win")
+    act("tabs:1024:2048", "win")
 
-    idle += [(ts, "w1:0:1", "p16F:0:1", "<", 4.0), (ts, "c3:0:1", "p16F:0:1", ">=", 4.0),
-             (ts, "w0:0:1", "p16F:0:1", "<", 2.0), (ts, "w2:0:1", "p16F:0:1", "==", 2.0, "*", 8192.0),
-             (ts, "w3:0:1", "p16F:0:1", "==", 3.0, "*", 2097152.0), (tt, "w4:0:1", "w0:0:1", "+", "w2:0:1"),
-             (ts, "w6:0:1", "p16F:0:1", "<", 8.0), (tt, "wcol:0:1", "w4:0:1", "+", "w3:0:1"), (ts, "w5:0:1", "p16F:0:1", ">=", 8.0),
+    idle += [(fill, "rsw", 1.0), (ts, "ckA:0:1", "ckp:0:1", "&", 3840), (ts, "ckA:1:2", "ckp:0:1", "&", 255), (fill, "rsw:0:256:8", 0.0),
+             (cp, "ckF:0:2", "ckA:0:2"), (ts, "c3:0:1", "p16F:0:1", ">=", 4.0, "*", 8192.0),
+             (ts, "ckL:2:128:16", "onesB:0:8", "*", "ckF:0:1"), (ts, "ckL:3:128:16", "onesB:0:8", "*", "ckF:1:2"),
+             (ts, "w2:0:1", "p16F:0:1", ">=", 2.0, "*", 8192.0),
+             (ts, "wS:0:1", "c3:0:1", "max", 1.0), (ts, "wcol:0:1", "w2:0:1", "max", 1.0),
+             (ts, "w6:0:1", "p16F:0:1", "<", 8.0), (ts, "w5:0:1", "p16F:0:1", ">=", 8.0),
              (tt, "oh8:0:8", "oh:0:8", "+", "oh:8:16")]
     cp("sF:0:1", "sdI:0:1")
     ts("hI:0:1", "sdI:0:1", ">>", 12)
-    ts("8|ya", "8|rkI:8:16", "*", 8192.0)
+    ts("8|ya", "8|rkI:0:8", "*", 16.0)
     ts("oT", "ckN", "+", "sF:0:1")
     ts("hF:0:1", "hI:0:1", "*", 64.0, "+", -BIG)
-    tt("8|yb", "8|ya", "+", "8|wc")
+    tt("8|yc:1:9", "8|ya", "+", "8|rkI:8:16")
     ts("oL", "oT", "&", 4095)
-    ts("lI:0:1", "sdI:0:1", "&", 4095)
-    tt("8|yc:1:9", "8|yb", "+", "8|rkI:0:8")
-    tt("oSq", "oL", "*", "oL")
-    cp("l1:0:1", "lI:0:1")
+    ts("lh:0:1", "sdI:0:1", "&", 3840)
     tt("8|dy", "8|yc:1:9", "-", "8|yc:0:8")
+    tt("oSq", "oL", "*", "oL")
+    ts("lh:1:2", "sdI:0:1", "&", 255)
+    ts("oL2", "oL", "*", 64.0, "+", -BIG)
     ts("oB0", "oSq", "+", "hF:0:1")
     mms("p3:0:8", [("8|e8", "8|dy")])
     act("dyS", "p3:0:8")
-    cp("h1:0:1", "hI:0:1")
-    fill("rsw", 1.0)
+    ts("lh:2:3", "hI:0:1", "&", 255)
+    ts("lh:3:4", "hI:0:1", "&", 3840)
     ts("oB", "oB0", ">>", 6, "&", 4095)
-    ts("oL2", "oL", "*", 64.0, "+", -BIG)
+    cp("lhF:0:3", "lh:0:3")
     run("S", lambda o, i, b: S.activation(o, i, AF.Abs, bias=b), "ohA", ["ohI", "n16:0:1"])
-    run("S", lambda o, i: S.activation(o, i, AF.Relu, bias=1.0, scale=-1.0), "oh", ["ohA"])
+    act("oh", "ohA", 1.0, -1.0, AF.Relu)
+    act("selB:15:144:16", "g9:0:9")
     tt("oSr", "oB", "*", "oB")
-    tt("l0:0:1", "lI:0:1", "-", "l1:0:1")
+    ts("lhF:3:4", "lh:3:4", "+", -2048.0)
+    for j, c in ((0, "lhF:0:1"), (1, "lhF:1:2"), (4, "lhF:3:4"), (5, "lhF:2:3")):
+        scaled("selX:%d:128:16" % j, "g9:0:8", c)
     tt("oA0", "oSr", "+", "oL2")
-    fill("rsw:0:256:8", 0.0)
-    tt("h0:0:1", "hI:0:1", "-", "h1:0:1")
+    ts("oB16", "oB", "*", 16.0, "+", 8.0)
+    gap()
     ts("oA", "oA0", ">>", 6, "&", 4095)
-    ts("selX:0:128:16", "g9:0:8", "*", "l1:0:1")
+    gap(2)
     for w in range(N):
         ts("st:%d:256:8" % w, "oA", ">=", 512.0 * w, "*", at("dyS", 1, w))
     ts("oW", "oA", ">>", 9)
+    gap()
     scan("yI", "rsw", "st")
-    ts("selX:1:128:16", "g9:0:8", "*", "l0:0:1")
-    ts("selX:4:128:16", "g9:0:8", "*", "h1:0:1")
-    ts("oTh", "yI:7:256:8", "&", 8191)
-    ts("oD", "yI:7:256:8", ">>", 13)
-    ts("selX:5:128:16", "g9:0:8", "*", "h0:0:1")
-    tt("oF", "oB", ">=", "oTh")
-    ts("ckA:0:1", "ckp:0:1", "&", 4095)
-    tt("oFd", "oF", "*", "oD")
-    cp("c1:0:1", "ckA:0:1")
-    tt("own", "oFd", "+", "oW")
-    cp("selB:15:144:16", "g9:0:9")
+    tt("oP", "oB16", "+", "oW")
+    gap()
+    tt("oM", "yI:7:256:8", "min", "oP")
+    gap(2)
+    ts("own", "oM", "&", 7)
+    gap(2)
     for q in range(N):
         ts(at("mq", 32, q), "own", "==", float(q))
-    tt("c0:0:1", "ckA:0:1", "-", "c1:0:1")
-    ts("ckL:2:128:16", "onesB:0:8", "*", "c1:0:1")
+    gap(2)
     scan("sc", "rs", "mq")
-    ts("ckL:3:128:16", "onesB:0:8", "*", "c0:0:1")
-    mms("p2:0:8", [("lt", "sc:31:256:32")])
+    mms("p2:0:8", [("onesB", "q8:0:8"), ("lt", "sc:31:256:32")])
     mms("p7", [("selX", "oh"), ("ckL", "kE")])
     act("be:1:32:4", "sc:31:256:32")
     cp("mqF", "mq")
-    tt("be:0:32:4", "p2:0:8", "+", "qc")
-    act("inX", "p7")
     gap()
-    tt("mqF:0:256:32", "mq:0:256:32", "+", "be:0:32:4")
+    tt("mqF:0:256:32", "mq:0:256:32", "+", "p2:0:8")
+    act("be:0:32:4", "p2:0:8")
+    act("inX", "p7")
     gap()
     scan("p1:0:256", "rs", "mqF")
     gap()
@@ -330,29 +325,39 @@ def rank_program(g, core, T, topo):
     gap()
     tt("b2", "p0:128:192", "+", "b4")
     gap()
-    tt("v", "b2:0:32", "+", "b2:32:64")
+    tt("v1", "b2:0:32", "+", "b2:32:64")
     gap()
-    cp("a16", "v")
-    gap()
+    ts("a16", "v1", "-", 1.0)
     send("r_be", lambda q: at("be", 4, q), at("beR", 4, me), "l_be")
-    scaled("selA", "selB", "w1:0:1")
-    scaled("selC", "selB", "c3:0:1")
-    act("tabs:1024:2048", "tabs:0:1024")
+    scaled("selP", "selB", "wS:0:1")
     act("tabs:2048:4096", "tabs:0:2048")
     cp("win@a16", "inX")
-    for out, sel in (("p4:0:64", "selA"), ("p5:0:64", "selC")):
-        mms(out, [("%s:%d:%d" % (sel, 15 - b, 143 - b), "win:%d:1024:16" % b) for b in range(16)])
+    mms("p4:0:64", [("selP:%d:%d" % (15 - b, 143 - b), "win:%d:1024:16" % b) for b in range(16)])
 
-    cp("alH", "aliI")
-    ts("thH", "thrI", ">>", 8)
-    ts("thL", "thrI", "&", 255)
-    tt("alL", "aliI", "-", "alH")
-    ts("thHb", "thH", "+", -8.0)
-    cp("thLb", "thL")
+    cp("p5:0:256", "aliI")
+    act("alH", "p5:0:256", -8.0, 1.0, AF.Relu)
+    ts("p6:0:256", "thrI", "+", -2048.0)
+    act("thH", "p6:0:256", -4.0)
     cp(at("beR", 4, me), at("be", 4, me))
-    for j, name in enumerate(("alL", "alH", "thLb", "thHb")):
+    cp(parts("rq", 0, 8), "p4:0:64")
+    send("r_rq", lambda q: block("rq", q), block("rr", me), "l_rq")
+    tt("alL", "p5:0:256", "-", "alH")
+    tt("thL", "p6:0:256", "-", "thH")
+    for j, name in ((1, "alH"), (3, "thH"), (0, "alL"), (2, "thL")):
         dma("Y", (T.tabs[j:128:16, :], X("tabs")[1]), name, "d_tab%d" % j, j)
+    Y.wait_ge(T.sem["l_rq"], count["l_rq"])
     dma("Y", "vecB", ext(T.vec), "d_vec")
+
+    ts("nm0", "beR:1:32:4", "*", -0.5, "+", 0.5 + float(128 * me))
+    ts("ha2", "beR:1:32:4", "*", 0.5, "+", -0.25)
+    tt("nm", "nm0", "-", "beR:0:32:4")
+    for r in range(N):
+        run("S", lambda o, i, b: S.activation(o, i, AF.Abs, bias=b), at("mT", 128, r), ["iotaS", at("nm", 1, r)])
+    gap(len(idle))
+    scaled("selT", "selB", "wcol:0:1")
+    cp(block("rr", me), block("rq", me))
+    for r in range(N):
+        ts(at("mask", 128, r), at("mT", 128, r), "<", at("ha2", 1, r), "*", float(2 ** (15 - r)))
     keep("idn", "onesB", [[-1, 128]], "==", 0, 1)
     keep("up8", "onesB", [[-1, 128]], "==", 8, 1)
     keep("dn8", "onesB", [[-1, 128]], "==", -8, 1)
@@ -363,149 +368,138 @@ def rank_program(g, core, T, topo):
     def counter(i):
         return float(1597 * (i + 1) % 4096)
 
-    def hashes(i0, i1, name):
-        n = i1 - i0
-
+    def hashes(i0, n):
         def r(tile):
             return R(tile, i0, n)
+        each = range(i0, i0 + n)
+        return ([(ts, R("hT", i), "xl", "+", counter(i)) for i in each] +
+                [(ts, r("hL"), r("hT"), "&", 4095), (tt, r("p0"), r("hL"), "*", r("hL"))] +
+                [(tt, R("hb", i), R("p0", i), "+", "H6") for i in each] +
+                [(ts, r("hB"), r("hb"), ">>", 6, "&", 4095), (tt, r("p1"), r("hB"), "*", r("hB")),
+                 (tt, r("ha"), r("p1"), "+", r("hL2")), (ts, r("hA"), r("ha"), ">>", 6, "&", 4095), (cp, r("e16"), r("hA")),
+                 (ts, r("p0"), r("hB"), "*", 8192.0, "+", 4096.0 - 16777216.0), (tt, r("pk"), r("p0"), "+", r("hA"))])
 
-        for i in range(i0, i1):
-            act(R("H6", i), "p5:0:64", -BIG, 64.0)
-        if i0 == 0:
-            for i in range(i1):
-                ts(R("hT", i), "p4:0:64", "+", counter(i))
-        ts(r("hL"), r("hT"), "&", 4095)
-        if i0 == 0:
-            for i in range(i1, TRY):
-                ts(R("hT", i), "p4:0:64", "+", counter(i))
-        for i in range(i0, i1):
-            act(R("hL2", i), "p4:0:64", 64.0 * counter(i) - BIG, 64.0)
-        q, rr, q0 = R("p6", 0, n), R("p3", 0, n), "p7:0:%d" % (64 * n)
-        gap()
-        tt(q, r("hL"), "*", r("hL"))
-        gap()
-        tt(r("hb"), q, "+", r("H6"))
-        gap()
-        ts(r("hB"), r("hb"), ">>", 6, "&", 4095)
-        gap()
-        tt(rr, r("hB"), "*", r("hB"))
-        ts(q0, r("hB"), "*", 8192.0, "+", 4096.0 - 16777216.0)
-        tt(r("ha"), rr, "+", r("hL2"))
-        gap()
-        ts(r("hA"), r("ha"), ">>", 6, "&", 4095)
-        gap()
-        for i in range(i0, i1):
-            tt(parts("rq" + name, 8 * (i - i0), 8 * (i - i0) + 8), R("p7", i - i0), "+", R("hA", i))
-        send("r_rq" + name, lambda q: block("rq" + name, q), block("rr" + name, me), "l_rq" + name)
-        idle.insert(0, (cp, block("rr" + name, me), block("rq" + name, me)))
-
-    hashes(*GROUPS[0], "0")
-    idle += [(ts, "ha2", "beR:1:32:4", "*", 0.5, "+", -0.25),
-             (ts, "nm0", "beR:1:32:4", "*", -0.5, "+", 0.5 + float(128 * me - 1)), (tt, "nm", "nm0", "-", "beR:0:32:4")]
-    hashes(*GROUPS[1], "1")
-    own1 = idle.pop(0)
-    gap(len(idle))
-    for r in range(N):
-        run("S", lambda o, i, b: S.activation(o, i, AF.Abs, bias=b), at("mT", 128, r), ["iotaS", at("nm", 1, r)])
-
-    def packed(i):
-        for j, (i0, i1) in enumerate(GROUPS):
-            if i0 <= i < i1:
-                return parts("rr%d" % j, 8 * (i - i0), 8 * (i - i0) + 8)
-
-    def places(i0, i1):
-        return [(ts, R("eI", i), packed(i), "&", 4095) for i in range(i0, i1)] + [(cp, R("e16", i), R("eI", i)) for i in range(i0, i1)]
-
-    def wrap(out, sel, src, i):
-        mms(out + ":0:64", [("%s:%d:%d" % (sel, 15 - b, 143 - b), "%s:%d:%d:16" % (src, 1024 * i + b, 1024 * i + 1024)) for b in range(16)])
+    def wrap(out, sel, src, a, n):
+        mms(out + ":0:%d" % (n // 16), [("%s:%d:%d" % (sel, 15 - b, 143 - b), "%s:%d:%d:16" % (src, a + b, a + n)) for b in range(16)])
 
     def bank(i):
-        return ("p2", "p6", "p7")[i % 3]
+        return ("p2", "p5")[i % 2]
+
+    def sbank(i):
+        return ("p3", "p4")[i % 2]
 
     def table(i):
-        wrap(bank(i), "selT", "tg", i)
+        wrap(bank(i), "selT", "tg", 1024 * i, 1024)
+
+    def look(i):
+        act(at("tg", 1024, i), "tabs@" + R("e16", i))
 
     def seen(i):
         tt(at("sg", 1024, i), "seenB@" + R("c16", i), "*", "mask")
-        wrap("p%d" % (3 + i % 3), "selB", "sg", i)
+        wrap(sbank(i), "selB", "sg", 1024 * i, 1024)
 
     def item(i):
-        ops = [(tt, R("xI", i), bank(i) + ":0:64", "min", packed(i)), (ts, R("cI", i), R("xI", i), "&", 4095)]
+        ops = [(tt, R("xI", i), bank(i) + ":0:64", "min", R("pk", i)), (ts, R("cI", i), R("xI", i), "&", 4095)]
         if i < TRY - 1:
             ops.append((cp, R("c16", i), R("cI", i)))
-            ops.append((ts, R("kI", i), R("cI", i), "+", 4096.0 * (TRY - 1 - i)))
+            ops.append((ts, R("p1", i), R("cI", i), "+", 4096.0 * (TRY - 1 - i)))
         return ops
 
     def known(j):
-        return [(cp, R("wI", j), "p%d:0:64" % (3 + j % 3)), (ts, R("sI", j), R("wI", j), "&", 1 << 15)]
+        return [(cp, R("wI", j), sbank(j) + ":0:64"), (ts, R("sI", j), R("wI", j), "&", 1 << 15)]
 
     def go(j):
-        k = "p%d" % (j % 2)
         if j == 0:
-            return [(tt, R("acc", 0), R("kI", 0), "-", R("sI", 0))]
-        return [(tt, k + ":0:64", R("kI", j), "-", R("sI", j)), (tt, R("acc", j), k + ":0:64", "max", R("acc", j - 1))]
+            return [(tt, R("acc", 0), R("p1", 0), "-", R("sI", 0))]
+        return [(tt, R("p0", j), R("p1", j), "-", R("sI", j)), (tt, R("acc", j), R("p0", j), "max", R("acc", j - 1))]
 
-    weave(places(*GROUPS[0]))
-    act("tg:0:512", "tabs@e16:0:32")
-    scaled("selT", "selB", "wcol:0:1")
-    cp("tg:512:1024", "tabs@e16:32:64")
+    x = parts("rr", 0, 8)
+    ts("xl", x, "&", 8191)
+    ts("xh", x, ">>", 13)
+    cp("xlF", "xl")
+    first = hashes(0, 1)
+    second = hashes(1, 1)
+    for i in range(TRY):
+        act(R("hL2", i), "xlF", 64.0 * counter(i) - BIG, 64.0)
+    weave(first[:1], second[:1], [(ts, "H6", "xh", "*", 64.0, "+", 131072.0 - BIG)])
+    weave(first[1:], second[1:])
+    look(0)
     table(0)
-    act(at("tg", 1024, 1), "tabs@" + R("e16", 1))
-    own1[0](*own1[1:])
-    for r in range(N):
-        ts(at("mask", 128, r), at("mT", 128, r), "<", at("ha2", 1, r), "*", float(2 ** (15 - r)))
+    look(1)
     table(1)
-    weave(item(0))
-    seen(0)
-    late = places(*GROUPS[1])
-    weave(late[0:4] + late[4:6])
+    for h in range(2):
+        mms(("p6", "p7")[h], [("idn", "mask:%d:%d" % (512 * h, 512 * h + 512))])
+    third, fourth = hashes(2, 2), hashes(4, 2)
+    weave(third, fourth[:-3], [None] * 8 + item(0))
     for i in (2, 3):
-        act(at("tg", 1024, i), "tabs@" + R("e16", i))
-    weave(item(1)[0:2], late[6:8])
-    weave(item(1)[2:])
-    for i in (4, 5):
-        act(at("tg", 1024, i), "tabs@" + R("e16", i))
+        look(i)
     table(2)
-    seen(1)
+    seen(0)
+    weave(item(1), fourth[-3:])
+    for i in (4, 5):
+        look(i)
     for out, a, c in (("wI0", "idn", "w6"), ("wU", "up8", "w6"), ("wI1", "idn", "w5"), ("wD", "dn8", "w5")):
         scaled(out, a, c + ":0:1")
-    for i in range(2, TRY - 1):
-        table(i + 1)
-        weave(go(i - 3) if i > 2 else [], item(i), known(i - 2))
+    for i in range(1, TRY - 2):
+        if i + 2 < TRY:
+            table(i + 2)
+        weave(item(i + 1), known(i - 2) if i > 1 else [], go(i - 3) if i > 2 else [])
+        if i == TRY - 3:
+            act("su", "seenB@" + R("c16", i + 1))
         seen(i)
-    weave(go(2), item(5), known(3))
-    weave(go(3)[:1])
-    cp(R("wI", 4), "p4:0:64")
-    tt(R("acc", 3), "p1:0:64", "max", R("acc", 2))
-    ts(R("sI", 4), R("wI", 4), "&", 1 << 15)
-    tt("a6", R("acc", 3), "max", R("cI", 5))
-    tt("p0:0:64", R("kI", 4), "-", R("sI", 4))
-    tt("aA", "p0:0:64", "max", "a6")
-    ts(R("acc", 4), "aA", "&", 4095)
-    cp("f16", R("acc", 4))
+    far = T.rank_of(off[0]) // 4
+    halves = (far, 1 - far)
+    weave(known(2), item(5), go(1))
+    for h in halves:
+        tt("sg:%d:%d" % (4096 + 512 * h, 4608 + 512 * h), "su:%d:%d" % (512 * h, 512 * h + 512), "*", ("p6", "p7")[h])
+    for h in halves:
+        wrap(("p3", "p2")[h], "selB", "sg", 4096 + 512 * h, 512)
+
+    def H(name, h):
+        return "%s:%d:%d" % (name, 32 * h, 32 * h + 32)
+
+    def final(h):
+        return [(cp, H("wL", h), ("p3", "p2")[h] + ":0:32"), (ts, H("sL", h), H("wL", h), "&", 1 << 15),
+                (tt, H("p0", h), "p1:%d:%d" % (256 + 32 * h, 288 + 32 * h), "-", H("sL", h)), (tt, H("aA", h), H("p0", h), "max", H("a6", h)),
+                (ts, H("r", h), H("aA", h), "&", 4095), (cp, H("f16", h), H("r", h)),
+                (cp, H("iH", h), H("r", h)), (tt, H("iL", h), H("r", h), "-", H("iH", h))]
 
     def features(q, r):
         out = "rspR:%d:%d" % (RW * me, RW * me + 128) if r == me else block("rsp", r, 0, 128)
         (act if q == "S" else cp)(out, "vecB@" + at("f16", 8, r))
 
+    def items(h):
+        b = ("p3", "p2")[h]
+        mms(b + ":64:96", [("wU", H("iH", h)), ("wI0", H("iL", h))])
+        mms(b + ":96:128", [("wD", H("iH", h)), ("wI1", H("iL", h))])
+
+    def itemcols(h):
+        for j in range(2):
+            cp((T["rsp"][:, 4 * h:4 * h + 4, 128 + 8 * j:136 + 8 * j], parts("rsp", 128 + 8 * j, 136 + 8 * j)[1][4 * h:4 * h + 4]),
+               ("p3", "p2")[h] + ":%d:%d" % (64 + 32 * j, 96 + 32 * j))
+
     order = [T.rank_of(c) for c in off + on] + [me]
-    cp("iH", R("acc", 4))
-    features("S", order[0])
-    features("V", order[2])
-    features("S", order[1])
-    tt("iL", R("acc", 4), "-", "iH")
-    features("V", order[3])
-    mms("p2:0:64", [("wU", "iH"), ("wI0", "iL")])
-    mms("p2:64:128", [("wD", "iH"), ("wI1", "iL")])
-    features("S", order[4])
-    features("V", order[5])
-    features("S", order[6])
-    for h in range(2):
-        cp(parts("rsp", 128 + 8 * h, 136 + 8 * h), "p2:%d:%d" % (64 * h, 64 * h + 64))
-    send("r_rsp", lambda q: block("rsp", q), at("rspR", RW, me), "l_rsp")
+    early, late = final(halves[0]), final(halves[1])
+    weave(known(3) + go(3) + [(tt, "a6", R("acc", 3), "max", R("cI", 5))], go(2), [None, None] + early[:3])
+    weave(early[3:6])
+    for r in order[:4]:
+        features("S", r)
+    weave(early[6:], late[:2])
+    items(halves[0])
+    weave(late[2:5])
+    itemcols(halves[0])
+    weave(late[5:])
+    items(halves[1])
+    send("r_rsp", lambda q: block("rsp", q), at("rspR", RW, me), "l_rsp", off)
+    features("V", order[4])
+    features("S", order[5])
+    features("V", order[6])
+    itemcols(halves[1])
+    send("r_rsp", lambda q: block("rsp", q), at("rspR", RW, me), "l_rsp", on)
     features("V", order[7])
     cp("rspR:%d:%d" % (RW * me + 128, RW * me + RW), block("rsp", me, 128, RW))
 
+    cp("v", "a16")
     ts("q1", "v", ">>", 7)
     ts("mm", "v", ">>", 4, "&", 7)
     ts("bl", "v", "&", 7)

from concourse.bass import DstId, RemoteDMATransfer
from concourse.mybir import AluOpType as A_, ActivationFunctionType as AF

N = 8
TRY = 6
RW = 144
BIG = float(1 << 23)
OPS = {"+": A_.add, "-": A_.subtract, "*": A_.mult, "min": A_.min, "max": A_.max, ">=": A_.is_ge, ">": A_.is_gt, "<": A_.is_lt,
       "==": A_.is_equal, ">>": A_.arith_shift_right, "&": A_.bitwise_and}

SMALL = {
    "bufI": ("int32", 8, "ckN 32 pI 8 p16I 8 sdI 8 hI 8 lh 8 ckp 8 ckA 8 rkI 16 oT 32 oL 32 oL2 32 oSq 32 oB0 32 oB 32 oSr 32 oA0 32 oA 32 "
             "oW 32 oB16 32 oP 32 oM 32 own 32 yI 256 v1 32 v 32 thrI 256 aliI 256 xl 64 xh 64 hT 384 hL 384 "
             "hb 384 hB 384 ha 384 hA 384 pk 384 xI 384 cI 384 wI 320 sI 320 acc 320 a6 64 aA 64 r 64 wL 64 sL 64 q1 32 "
             "q16 32 ps 32 mm 32 cq 32 cl 32 bl 32 b8I 32 mb 32"),
    "bufF": ("float32", 8, "ones 128 p16F 8 n16 8 e8a 128 e8 128 g9a 16 g9 16 w2 8 w5 8 w6 8 wcol 8 c3 8 wS 8 lhF 8 ckF 8 "
             "ya 8 yc 16 dy 8 dyS 8 sF 8 hF 8 st 256 mqF 256 be 32 beR 32 b8 128 b4 64 "
             "b2 64 xlF 64 H6 64 hL2 384 ha2 8 nm 8 nm0 8 mT 1024 q4k 32 ch1 32"),
    "bufB": ("bfloat16", 16, "onesB 128 ones5 512 lta 128 lt 128 selB 144 selT 144 selP 144 selX 128 ckL 128 "
             "idn 128 up8 128 dn8 128 wI0 128 wI1 128 wU 128 wD 128 iH 64 iL 64 oh8 16 q8 16 "
             "iotaS 128 ohI 512 ohA 512 oh 512 kE 512 inX 512 rs 256 rsw 256 mq 256 sc 256 "
             "alH 256 alL 256 thH 256 thL 256 win 1024 mask 1024 m2 512 cm 512 ysb 512"),
    "bufU": ("uint16", 16, "a16 32 e16 384 c16 320 f16 64 l16 96"),
}
SCRATCH = {}
TILES = {}
for _buf, (_type, _step, _list) in SMALL.items():
    _at, _w = 0, _list.split()
    for _n, _c in zip(_w[0::2], _w[1::2]):
        TILES[_n] = (_buf, _at, int(_c))
        _at += -(-int(_c) // _step) * _step
    SCRATCH[_buf] = ("sbuf", [128, _at], _type)
for _n, _c, _type in (("seenB", 4096, "bfloat16"), ("vecB", 4096, "bfloat16"), ("tabs", 4096, "bfloat16"),
                      ("tg", 6144, "bfloat16"), ("sg", 5120, "bfloat16"), ("su", 1024, "bfloat16"), ("rspR", N * RW, "bfloat16")):
    SCRATCH[_n] = ("sbuf", [128, _c], _type)
    TILES[_n] = (_n, 0, _c)
for _j in range(8):
    SCRATCH["p%d" % _j] = ("psum", [128, 512], "float32")
    TILES["p%d" % _j] = ("p%d" % _j, 0, 512)
BLOCKS = {"rsp": RW, "rq": 8, "rr": 8}
for _n, _c in BLOCKS.items():
    SCRATCH[_n] = ("sbuf", [128, N, _c], "bfloat16" if _n == "rsp" else "int32")
SEMAPHORES = ("sv ss sp sg d_sd d_rk d_thr d_ali d_seen d_vec d_tab0 d_tab1 d_tab2 d_tab3 d_y d_ch "
              "l_be l_rq l_rsp r_be r_rq r_rsp").split()


def engine_plan(core, T, topo):
    off = [c for c in T.cores if topo.chip(c) != topo.chip(core)]
    on = [c for c in T.cores if topo.chip(c) == topo.chip(core) and c != core]
    plan = {}
    pool = topo.engines(core, off[0])
    rest = [e for e in topo.engines(core, on[0]) if e not in pool]
    for cores, engines in ((off, pool), (on, rest)):
        n = 1
        while 2 * n * len(cores) <= len(engines):
            n *= 2
        at = 0
        for j, c in enumerate(cores):
            m = n
            if len(engines) - at - 2 * n >= n * (len(cores) - j - 1):
                m = 2 * n
            plan[c] = engines[at:at + m]
            at += m
    return plan, off, on


def rank_program(g, core, T, topo):
    me = T.rank_of(core)
    if me is None:
        return
    queues = {"V": (g.vector, "sv"), "S": (g.scalar, "ss"), "P": (g.tensor, "sp"), "G": (g, "sg"), "Y": (g.sync, None)}
    V, S, P, Y = g.vector, g.scalar, g.tensor, g.sync
    count, waited, past = {}, {q: {} for q in queues}, {}

    def X(spec):
        if not isinstance(spec, str):
            return spec
        if "@" in spec:
            w, o = spec.split("@")
            (wa, wr), (oa, orr) = X(w), X(o)
            return wa.indirect(oa), wr + orr
        rows, name = (8, spec[2:]) if spec[:2] == "8|" else (128, spec)
        f = name.split(":")
        buf, at, n = TILES[f[0]]
        a, b, st = (int(f[1]), int(f[2]), int(f[3]) if len(f) > 3 else 1) if len(f) > 1 else (0, n, 1)
        return T[buf][0:rows, at + a:at + b:st], [(buf, at + a, at + b, st)]

    def meet(p, o, own):
        if p[0][0] == "p" and not own:
            return True
        if p[1] >= o[2] or o[1] >= p[2]:
            return False
        return (p[3] == 1 and o[3] == 1) or bool(set(range(p[1], p[2], p[3])) & set(range(o[1], o[2], o[3])))

    def need(q, reads, writes, part=None):
        tok, mine = {}, queues[q][1]
        for places, wr in ((reads, False), (writes, True)):
            for p in places:
                for o, t, is_w, pt in past.get(p[0], []):
                    if (is_w or wr or (p[0][0] == "p" and t[0] != mine)) and tok.get(t[0], 0) < t[1] \
                            and meet(p, o, t[0] == mine) and (pt is None or part is None or pt == part):
                        tok[t[0]] = t[1]
        for s in sorted(tok):
            if waited[q].get(s, 0) < tok[s]:
                queues[q][0].wait_ge(T.sem[s], tok[s])
                waited[q][s] = tok[s]

    def note(tok, reads, writes, part=None):
        for places, w in ((reads, False), (writes, True)):
            for p in places:
                past.setdefault(p[0], []).append((p, tok, w, part))

    def run(q, call, out, ins, *more):
        oa, ow = X(out)
        reads, args = [], []
        for i in ins:
            if isinstance(i, (str, tuple)):
                a, r = X(i)
                args.append(a)
                reads = reads + r
            else:
                args.append(i)
        need(q, reads, ow)
        s = queues[q][1]
        count[s] = count.get(s, 0) + 1
        call(oa, *args, *more).then_inc(T.sem[s], 1)
        note((s, count[s]), reads, ow)

    def ts(out, a, op, s1, op2=None, s2=None):
        run("V", V.tensor_scalar, out, [a, s1, s2], *([OPS[op]] if op2 is None else [OPS[op], OPS[op2]]))

    def tt(out, a, op, b):
        run("V", V.tensor_tensor, out, [a, b], OPS[op])

    def cp(out, a):
        run("V", V.tensor_copy, out, [a])

    def fill(out, c):
        run("V", V.memset, out, [], c)

    def scan(out, a, b):
        run("V", V.tensor_tensor_scan, out, [a, b], 0.0, A_.mult, A_.add)

    idle = []

    def gap(k=1):
        for _ in range(k):
            if idle:
                c = idle.pop(0)
                c[0](*c[1:])

    def weave(*chains):
        for j in range(max(len(c) for c in chains)):
            for c in chains:
                if j < len(c) and c[j]:
                    c[j][0](*c[j][1:])

    def act(out, a, bias=0.0, scale=1.0, func=AF.Copy):
        run("S", lambda o, i: S.activation(o, i, func, bias=bias, scale=scale), out, [a])

    def scaled(out, a, by):
        run("S", lambda o, i, c: S.activation(o, i, AF.Copy, scale=c), out, [a, by])

    def iota(out, pattern, base, cm, exact=False):
        run("G", lambda o: g.iota(o, pattern, base, cm) if exact else
            g.iota(o, pattern, base, cm, allow_small_or_imprecise_dtypes=True), out, [])

    def keep(out, a, pattern, op, base, cm):
        run("G", lambda o, i: g.affine_select(o, i, pattern, OPS[op], 0.0, base, cm), out, [a])

    def mms(out, pairs):
        def call(o, *args):
            for j in range(0, len(args), 2):
                last = P.matmul(o, args[j], args[j + 1], j == 0, j == len(args) - 2)
            return last
        run("P", call, out, [x for p in pairs for x in p])

    def dma(q, out, in_, sem, part=None):
        (oa, ow), (ia, ir) = X(out), X(in_)
        need(q, ir, ow, part)
        queues[q][0].dma_start(oa, ia).then_inc(T.sem[sem], 16)
        count[sem] = count.get(sem, 0) + 16
        note((sem, count[sem]), ir, ow, part)

    plan, off, on = engine_plan(core, T, topo)

    def send(sem, src, dst, local, cores=None):
        tr = []
        for c in cores or off + on:
            rid, pnc, _s = topo.addr(c)
            a, r = X(src(T.rank_of(c)))
            need("G", r, [])
            m = 0
            for e in plan[c]:
                m |= 1 << e
            tr.append(RemoteDMATransfer(dst_ids=[DstId(rid=rid, pnc=pnc)], dma_engine_mask=m, remote_sem=T.sem[sem],
                                        srcs=[a], dsts=[X(dst)[0]], alu_op=0))
            count[local] = count.get(local, 0) + len(plan[c])
        g.remote_dma_fused(tr, local_sem=T.sem[local])

    def block(name, r, a=0, b=None):
        w = BLOCKS[name]
        b = w if b is None else b
        return T[name][:, r, a:b], [(name, w * r + a, w * r + b, 1)]

    def parts(name, a, b):
        w = BLOCKS[name]
        return T[name][:, :, a:b], [(name, w * r + a, w * r + b, 1) for r in range(N)]

    def landing(piece, sem):
        count[sem] = sum(len(engine_plan(c, T, topo)[0][core]) for c in T.cores if c != core)
        for r in range(N):
            if r != me:
                note((sem, count[sem]), [], X(piece(r))[1])

    def ext(t):
        return (t[:], [])

    def at(name, w, i):
        return "%s:%d:%d" % (name, w * i, w * i + w)

    landing(lambda r: at("beR", 4, r), "r_be")
    landing(lambda r: block("rr", r), "r_rq")
    landing(lambda r: at("rspR", RW, r), "r_rsp")

    dma("Y", "sdI:0:1", ext(T.sd), "d_sd")
    dma("S", "8|rkI", ext(T.rk), "d_rk")
    dma("Y", "thrI", ext(T.thr), "d_thr")
    dma("Y", "aliI", ext(T.ali), "d_ali")
    dma("Y", "seenB", ext(T.seen), "d_seen")

    for name, c in (("ones", 1.0), ("win", 0.0), ("onesB", 1.0), ("ones5", 1.0), ("selB", 0.0), ("selX", 0.0), ("ckL", 0.0),
                    ("yc", 0.0), ("be", 0.0), ("rs", 1.0)):
        fill(name, c)
    step = 1597 * (TRY + 1)
    iota("ckN", [[step, 32]], -int(BIG), 0, True)
    iota("pI:0:1", [[0, 1]], 0, 1, True)
    iota("ckp:0:1", [[0, 1]], 0, step, True)
    iota("q8:0:8", [[1, 8]], 0, 0)
    keep("8|e8a", "8|ones", [[1, 128]], ">=", 0, -16)
    keep("8|e8", "8|e8a", [[-1, 128]], ">=", 15, 16)
    keep("g9a:0:9", "ones:0:9", [[-16, 9]], ">=", 0, 1)
    keep("g9:0:9", "g9a:0:9", [[16, 9]], ">=", 15, -1)
    iota("ohI", [[0, 32], [1, 16]], 0, 0)
    keep("lta", "onesB", [[16, 8], [1, 16]], ">", 0, -1)
    keep("lt", "lta", [[-16, 8], [0, 16]], ">=", 0, 1)
    keep("kE", "ones5", [[1, 32], [0, 16]], "==", 0, -1)
    iota("iotaS", [[1, 128]], 0, 0)
    ts("p16I:0:1", "pI:0:1", "&", 15)
    fill("rs:0:256:32", 0.0)
    cp("p16F:0:1", "p16I:0:1")
    ts("n16:0:1", "p16F:0:1", "*", -1.0)
    act("tabs:0:1024", "win")
    act("tabs:1024:2048", "win")

    idle += [(fill, "rsw", 1.0), (ts, "ckA:0:1", "ckp:0:1", "&", 3840), (ts, "ckA:1:2", "ckp:0:1", "&", 255), (fill, "rsw:0:256:8", 0.0),
             (cp, "ckF:0:2", "ckA:0:2"), (ts, "c3:0:1", "p16F:0:1", ">=", 4.0, "*", 8192.0),
             (ts, "ckL:2:128:16", "onesB:0:8", "*", "ckF:0:1"), (ts, "ckL:3:128:16", "onesB:0:8", "*", "ckF:1:2"),
             (ts, "w2:0:1", "p16F:0:1", ">=", 2.0, "*", 8192.0),
             (ts, "wS:0:1", "c3:0:1", "max", 1.0), (ts, "wcol:0:1", "w2:0:1", "max", 1.0),
             (ts, "w6:0:1", "p16F:0:1", "<", 8.0), (ts, "w5:0:1", "p16F:0:1", ">=", 8.0),
             (tt, "oh8:0:8", "oh:0:8", "+", "oh:8:16")]
    cp("sF:0:1", "sdI:0:1")
    ts("hI:0:1", "sdI:0:1", ">>", 12)
    ts("8|ya", "8|rkI:0:8", "*", 16.0)
    ts("oT", "ckN", "+", "sF:0:1")
    ts("hF:0:1", "hI:0:1", "*", 64.0, "+", -BIG)
    tt("8|yc:1:9", "8|ya", "+", "8|rkI:8:16")
    ts("oL", "oT", "&", 4095)
    ts("lh:0:1", "sdI:0:1", "&", 3840)
    tt("8|dy", "8|yc:1:9", "-", "8|yc:0:8")
    tt("oSq", "oL", "*", "oL")
    ts("lh:1:2", "sdI:0:1", "&", 255)
    ts("oL2", "oL", "*", 64.0, "+", -BIG)
    ts("oB0", "oSq", "+", "hF:0:1")
    mms("p3:0:8", [("8|e8", "8|dy")])
    act("dyS", "p3:0:8")
    ts("lh:2:3", "hI:0:1", "&", 255)
    ts("lh:3:4", "hI:0:1", "&", 3840)
    ts("oB", "oB0", ">>", 6, "&", 4095)
    cp("lhF:0:3", "lh:0:3")
    run("S", lambda o, i, b: S.activation(o, i, AF.Abs, bias=b), "ohA", ["ohI", "n16:0:1"])
    act("oh", "ohA", 1.0, -1.0, AF.Relu)
    act("selB:15:144:16", "g9:0:9")
    tt("oSr", "oB", "*", "oB")
    ts("lhF:3:4", "lh:3:4", "+", -2048.0)
    for j, c in ((0, "lhF:0:1"), (1, "lhF:1:2"), (4, "lhF:3:4"), (5, "lhF:2:3")):
        scaled("selX:%d:128:16" % j, "g9:0:8", c)
    tt("oA0", "oSr", "+", "oL2")
    ts("oB16", "oB", "*", 16.0, "+", 8.0)
    gap()
    ts("oA", "oA0", ">>", 6, "&", 4095)
    gap(2)
    for w in range(N):
        ts("st:%d:256:8" % w, "oA", ">=", 512.0 * w, "*", at("dyS", 1, w))
    ts("oW", "oA", ">>", 9)
    gap()
    scan("yI", "rsw", "st")
    tt("oP", "oB16", "+", "oW")
    gap()
    tt("oM", "yI:7:256:8", "min", "oP")
    gap(2)
    ts("own", "oM", "&", 7)
    gap(2)
    for q in range(N):
        ts(at("mq", 32, q), "own", "==", float(q))
    gap(2)
    scan("sc", "rs", "mq")
    mms("p2:0:8", [("onesB", "q8:0:8"), ("lt", "sc:31:256:32")])
    mms("p7", [("selX", "oh"), ("ckL", "kE")])
    act("be:1:32:4", "sc:31:256:32")
    cp("mqF", "mq")
    gap()
    tt("mqF:0:256:32", "mq:0:256:32", "+", "p2:0:8")
    act("be:0:32:4", "p2:0:8")
    act("inX", "p7")
    gap()
    scan("p1:0:256", "rs", "mqF")
    gap()
    tt("p0:0:128", "p1:0:128", "*", "mq:0:128")
    tt("b8", "p1:128:256", "*", "mq:128:256")
    gap()
    tt("p0:128:192", "p0:0:64", "+", "b8:0:64")
    tt("b4", "p0:64:128", "+", "b8:64:128")
    gap()
    tt("b2", "p0:128:192", "+", "b4")
    gap()
    tt("v1", "b2:0:32", "+", "b2:32:64")
    gap()
    ts("a16", "v1", "-", 1.0)
    send("r_be", lambda q: at("be", 4, q), at("beR", 4, me), "l_be")
    scaled("selP", "selB", "wS:0:1")
    act("tabs:2048:4096", "tabs:0:2048")
    cp("win@a16", "inX")
    mms("p4:0:64", [("selP:%d:%d" % (15 - b, 143 - b), "win:%d:1024:16" % b) for b in range(16)])

    cp("p5:0:256", "aliI")
    act("alH", "p5:0:256", -8.0, 1.0, AF.Relu)
    ts("p6:0:256", "thrI", "+", -2048.0)
    act("thH", "p6:0:256", -4.0)
    cp(at("beR", 4, me), at("be", 4, me))
    cp(parts("rq", 0, 8), "p4:0:64")
    send("r_rq", lambda q: block("rq", q), block("rr", me), "l_rq")
    tt("alL", "p5:0:256", "-", "alH")
    tt("thL", "p6:0:256", "-", "thH")
    for j, name in ((1, "alH"), (3, "thH"), (0, "alL"), (2, "thL")):
        dma("Y", (T.tabs[j:128:16, :], X("tabs")[1]), name, "d_tab%d" % j, j)
    Y.wait_ge(T.sem["l_rq"], count["l_rq"])
    dma("Y", "vecB", ext(T.vec), "d_vec")

    ts("nm0", "beR:1:32:4", "*", -0.5, "+", 0.5 + float(128 * me))
    ts("ha2", "beR:1:32:4", "*", 0.5, "+", -0.25)
    tt("nm", "nm0", "-", "beR:0:32:4")
    for r in range(N):
        run("S", lambda o, i, b: S.activation(o, i, AF.Abs, bias=b), at("mT", 128, r), ["iotaS", at("nm", 1, r)])
    gap(len(idle))
    scaled("selT", "selB", "wcol:0:1")
    cp(block("rr", me), block("rq", me))
    for r in range(N):
        ts(at("mask", 128, r), at("mT", 128, r), "<", at("ha2", 1, r), "*", float(2 ** (15 - r)))
    keep("idn", "onesB", [[-1, 128]], "==", 0, 1)
    keep("up8", "onesB", [[-1, 128]], "==", 8, 1)
    keep("dn8", "onesB", [[-1, 128]], "==", -8, 1)

    def R(name, i, n=1):
        return "%s:%d:%d" % (name, 64 * i, 64 * i + 64 * n)

    def counter(i):
        return float(1597 * (i + 1) % 4096)

    def hashes(i0, n):
        def r(tile):
            return R(tile, i0, n)
        each = range(i0, i0 + n)
        return ([(ts, R("hT", i), "xl", "+", counter(i)) for i in each] +
                [(ts, r("hL"), r("hT"), "&", 4095), (tt, r("p0"), r("hL"), "*", r("hL"))] +
                [(tt, R("hb", i), R("p0", i), "+", "H6") for i in each] +
                [(ts, r("hB"), r("hb"), ">>", 6, "&", 4095), (tt, r("p1"), r("hB"), "*", r("hB")),
                 (tt, r("ha"), r("p1"), "+", r("hL2")), (ts, r("hA"), r("ha"), ">>", 6, "&", 4095), (cp, r("e16"), r("hA")),
                 (ts, r("p0"), r("hB"), "*", 8192.0, "+", 4096.0 - 16777216.0), (tt, r("pk"), r("p0"), "+", r("hA"))])

    def wrap(out, sel, src, a, n):
        mms(out + ":0:%d" % (n // 16), [("%s:%d:%d" % (sel, 15 - b, 143 - b), "%s:%d:%d:16" % (src, a + b, a + n)) for b in range(16)])

    def bank(i):
        return ("p2", "p5")[i % 2]

    def sbank(i):
        return ("p3", "p4")[i % 2]

    def table(i):
        wrap(bank(i), "selT", "tg", 1024 * i, 1024)

    def look(i):
        act(at("tg", 1024, i), "tabs@" + R("e16", i))

    def seen(i):
        tt(at("sg", 1024, i), "seenB@" + R("c16", i), "*", "mask")
        wrap(sbank(i), "selB", "sg", 1024 * i, 1024)

    def item(i):
        ops = [(tt, R("xI", i), bank(i) + ":0:64", "min", R("pk", i)), (ts, R("cI", i), R("xI", i), "&", 4095)]
        if i < TRY - 1:
            ops.append((cp, R("c16", i), R("cI", i)))
            ops.append((ts, R("p1", i), R("cI", i), "+", 4096.0 * (TRY - 1 - i)))
        return ops

    def known(j):
        return [(cp, R("wI", j), sbank(j) + ":0:64"), (ts, R("sI", j), R("wI", j), "&", 1 << 15)]

    def go(j):
        if j == 0:
            return [(tt, R("acc", 0), R("p1", 0), "-", R("sI", 0))]
        return [(tt, R("p0", j), R("p1", j), "-", R("sI", j)), (tt, R("acc", j), R("p0", j), "max", R("acc", j - 1))]

    x = parts("rr", 0, 8)
    ts("xl", x, "&", 8191)
    ts("xh", x, ">>", 13)
    cp("xlF", "xl")
    first = hashes(0, 1)
    second = hashes(1, 1)
    for i in range(TRY):
        act(R("hL2", i), "xlF", 64.0 * counter(i) - BIG, 64.0)
    weave(first[:1], second[:1], [(ts, "H6", "xh", "*", 64.0, "+", 131072.0 - BIG)])
    weave(first[1:], second[1:])
    look(0)
    table(0)
    look(1)
    table(1)
    for h in range(2):
        mms(("p6", "p7")[h], [("idn", "mask:%d:%d" % (512 * h, 512 * h + 512))])
    third, fourth = hashes(2, 2), hashes(4, 2)
    weave(third, fourth[:-3], [None] * 8 + item(0))
    for i in (2, 3):
        look(i)
    table(2)
    seen(0)
    weave(item(1), fourth[-3:])
    for i in (4, 5):
        look(i)
    for out, a, c in (("wI0", "idn", "w6"), ("wU", "up8", "w6"), ("wI1", "idn", "w5"), ("wD", "dn8", "w5")):
        scaled(out, a, c + ":0:1")
    for i in range(1, TRY - 2):
        if i + 2 < TRY:
            table(i + 2)
        weave(item(i + 1), known(i - 2) if i > 1 else [], go(i - 3) if i > 2 else [])
        if i == TRY - 3:
            act("su", "seenB@" + R("c16", i + 1))
        seen(i)
    far = T.rank_of(off[0]) // 4
    halves = (far, 1 - far)
    weave(known(2), item(5), go(1))
    for h in halves:
        tt("sg:%d:%d" % (4096 + 512 * h, 4608 + 512 * h), "su:%d:%d" % (512 * h, 512 * h + 512), "*", ("p6", "p7")[h])
    for h in halves:
        wrap(("p3", "p2")[h], "selB", "sg", 4096 + 512 * h, 512)

    def H(name, h):
        return "%s:%d:%d" % (name, 32 * h, 32 * h + 32)

    def final(h):
        return [(cp, H("wL", h), ("p3", "p2")[h] + ":0:32"), (ts, H("sL", h), H("wL", h), "&", 1 << 15),
                (tt, H("p0", h), "p1:%d:%d" % (256 + 32 * h, 288 + 32 * h), "-", H("sL", h)), (tt, H("aA", h), H("p0", h), "max", H("a6", h)),
                (ts, H("r", h), H("aA", h), "&", 4095), (cp, H("f16", h), H("r", h)),
                (cp, H("iH", h), H("r", h)), (tt, H("iL", h), H("r", h), "-", H("iH", h))]

    def features(q, r):
        out = "rspR:%d:%d" % (RW * me, RW * me + 128) if r == me else block("rsp", r, 0, 128)
        (act if q == "S" else cp)(out, "vecB@" + at("f16", 8, r))

    def items(h):
        b = ("p3", "p2")[h]
        mms(b + ":64:96", [("wU", H("iH", h)), ("wI0", H("iL", h))])
        mms(b + ":96:128", [("wD", H("iH", h)), ("wI1", H("iL", h))])

    def itemcols(h):
        for j in range(2):
            cp((T["rsp"][:, 4 * h:4 * h + 4, 128 + 8 * j:136 + 8 * j], parts("rsp", 128 + 8 * j, 136 + 8 * j)[1][4 * h:4 * h + 4]),
               ("p3", "p2")[h] + ":%d:%d" % (64 + 32 * j, 96 + 32 * j))

    order = [T.rank_of(c) for c in off + on] + [me]
    early, late = final(halves[0]), final(halves[1])
    weave(known(3) + go(3) + [(tt, "a6", R("acc", 3), "max", R("cI", 5))], go(2), [None, None] + early[:3])
    weave(early[3:6])
    for r in order[:4]:
        features("S", r)
    weave(early[6:], late[:2])
    items(halves[0])
    weave(late[2:5])
    itemcols(halves[0])
    weave(late[5:])
    items(halves[1])
    send("r_rsp", lambda q: block("rsp", q), at("rspR", RW, me), "l_rsp", off)
    features("V", order[4])
    features("S", order[5])
    features("V", order[6])
    itemcols(halves[1])
    send("r_rsp", lambda q: block("rsp", q), at("rspR", RW, me), "l_rsp", on)
    features("V", order[7])
    cp("rspR:%d:%d" % (RW * me + 128, RW * me + RW), block("rsp", me, 128, RW))

    cp("v", "a16")
    ts("q1", "v", ">>", 7)
    ts("mm", "v", ">>", 4, "&", 7)
    ts("bl", "v", "&", 7)
    ts("b8I", "v", "&", 8)
    ts("q16", "q1", "*", float(RW - 128))
    ts("cq", "q1", "*", float(RW), "+", 128.0)
    ts("q4k", "q1", "*", 4096.0)
    tt("mb", "mm", "+", "b8I")
    tt("ps", "v", "+", "q16")
    cp("l16:64:96", "bl")
    tt("cl", "cq", "+", "mb")
    cp("l16:0:32", "ps")
    cp("l16:32:64", "cl")
    cp("m2", "oh8:0:8@l16:64:96")

    act("ysb", "rspR@l16:0:32")
    dma("Y", ext(T.y), "ysb", "d_y")
    tt("cm", "rspR@l16:32:64", "*", "m2")
    mms("p7:0:32", [("selB:%d:%d" % (15 - u, 143 - u), "cm:%d:512:16" % u) for u in range(16)])
    tt("ch1", "p7:0:32", "+", "q4k")
    dma("S", ext(T.chosen), "ch1", "d_ch")
    for s in SEMAPHORES:
        if count.get(s, 0) > waited["G"].get(s, 0):
            g.wait_ge(T.sem[s], count[s])
